import numpy as np, ml_dtypes
CORES = [48,51,52,55]
N = 4
BF = ml_dtypes.bfloat16
def gentries(a):
    return np.ascontiguousarray(a.reshape(8, 16, -1).transpose(0, 2, 1)).reshape(8, -1)
def gtable(e):
    e = np.asarray(e); return np.ascontiguousarray(e.reshape(8, -1, 16).transpose(0, 2, 1)).reshape(128, -1).astype(np.int32)
M, Q, V, TOP = 2048, 256, 8, 15
WT = 255
def far_maps(rng):
    p = np.argsort(rng.random((N, 8, M)), axis=-1)
    return np.where(rng.random(p.shape) < 0.125, rng.integers(0, M, p.shape), p).astype(np.int32)
def lists(a):
    return np.stack([gtable(u) for u in a])
def setup_inputs(rng):
    return {"nx": far_maps(rng), "w": np.floor((WT + 1) * rng.random((N, 8, M)) ** 32).astype(np.int32), "x": lists(rng.integers(0, M, (N, 8, Q))), "e": lists(rng.integers(0, TOP + 1, (N, 8, V * Q)))}
def setup_inputs_ends(rng):
    d = setup_inputs(rng); k = rng.choice(np.array([0, TOP]), (N, 8, V, Q))
    k[:, :, :, 0] = 0; k[:, :, :, 1] = TOP; k[:, :, :, Q - 1] = 0; k[:, :, V - 1, Q - 1] = TOP
    d["e"] = lists(k.reshape(N, 8, V * Q))
    w = np.where(rng.random((N, 8, M)) < 0.015625, WT, 0); w[:, 0] = WT; d["w"] = w.astype(np.int32)
    return d
def setup_inputs_still(rng):
    d = setup_inputs(rng); a = np.array(d["nx"]); s = int(rng.integers(0, 4)); p = np.arange(M)
    for r in range(N):
        h = (r + s) % 4; c = rng.choice(np.arange(2, M - 1), 8, replace=False)
        if h == 0:
            a[r] = p
        elif h == 1:
            c[0] = 0; c[1] = M - 1; a[r] = rng.permutation(c)[:, None]
        elif h == 2:
            c[0] = 1; c[1] = M - 1; a[r] = (p + rng.permutation(c)[:, None]) % M
        else:
            c[0] = 1; c[1] = M - 1; a[r] = p ^ rng.permutation(c)[:, None]
    d["nx"] = a; return d
def setup_inputs_alike(rng):
    d = setup_inputs(rng); k = rng.integers(0, TOP + 1, (N, 8, V, Q // 2))
    z = np.where((np.arange(N)[:, None] + np.arange(8)) % 2 == 0, M - 1, 0)
    d["x"] = lists(np.repeat(z[:, :, None], Q, axis=2)); d["e"] = lists(np.concatenate([k, k], -1).reshape(N, 8, V * Q)); return d
def setup_inputs_spread(rng):
    d = setup_inputs(rng)
    d["nx"] = np.floor(M * rng.random((N, 8, M)) ** 3).astype(np.int32)
    d["w"] = np.floor((WT + 1) * rng.random((N, 8, M)) ** 16).astype(np.int32)
    d["x"] = lists(np.floor(M * rng.random((N, 8, Q)) ** 2)); d["e"] = lists(np.floor((TOP + 1) * rng.random((N, 8, V * Q)) ** 3)); return d
def check_inputs(d):
    bad = []
    for name, top in (("nx", M - 1), ("w", WT), ("x", M - 1), ("e", TOP)):
        if np.min(d[name]) < 0 or np.max(d[name]) > top: bad.append("range of " + name)
    return bad
def reference(nx, w, x, e):
    last = np.zeros((N, 128, Q // 16), np.int32); peak = np.zeros((N, 128, Q // 16), np.int32); g = np.arange(8)[:, None]
    for r in range(N):
        p = gentries(x[r]).astype(np.int64); k = gentries(e[r]).reshape(8, V, Q); s = np.zeros((8, Q), np.int64)
        for t in range(V):
            q = (r + t) % N
            for i in range(TOP):
                go = i < k[:, t]
                s = np.maximum(s, np.where(go, w[q][g, p], 0))
                p = np.where(go, nx[q][g, p], p)
        last[r] = gtable(p); peak[r] = gtable(s)
    return {"last": np.asarray(last, np.float32), "peak": np.asarray(peak, np.float32)}

@@ -1,0 +1,477 @@
+import numpy as np
+from concourse.bass import DstId, RemoteDMATransfer
+from concourse.mybir import dt, AluOpType, ActivationFunctionType
+
+ND = 40
+SCRATCH = {
+    "srcA": ("dram", [4, 128, 64], "int32"), "srcE": ("dram", [4, 128, 32], "int32"), "srcX": ("dram", [4, 128, 4], "int32"),
+    "landA": ("dram", [4, 128, 64], "int32"), "landE": ("dram", [4, 128, 32], "int32"), "landX": ("dram", [4, 128, 4], "int32"),
+    "landO": ("dram", [4, 128, 32], "float32"),
+    "s2r": ("sbuf", [128, 512], "int32"), "s2f": ("sbuf", [128, 512], "float16"), "l1r": ("sbuf", [128, 128], "int32"), "l1f": ("sbuf", [128, 128], "float16"),
+    "ep": ("sbuf", [128, 2, 64], "int32"), "ei": ("sbuf", [128, 128], "int32"), "fi": ("sbuf", [128, 128], "int32"), "ki": ("sbuf", [128, 128], "int32"),
+    "fb": ("sbuf", [128, 128], "bfloat16"), "off": ("sbuf", [128, 128], "float16"), "xr": ("sbuf", [128, 16], "int32"), "xe": ("sbuf", [128, 16], "int32"),
+    "t0": ("sbuf", [128, 2048], "bfloat16"), "t1": ("sbuf", [128, 2048], "bfloat16"), "tab": ("sbuf", [128, 10240], "bfloat16"),
+    "ga": ("sbuf", [128, 2048], "bfloat16"), "gb": ("sbuf", [128, 2048], "bfloat16"), "c4a": ("sbuf", [128, 640], "bfloat16"),
+    "l1": ("sbuf", [128, 128], "uint16"), "l2": ("sbuf", [128, 128], "uint16"), "l4": ("sbuf", [128, 128], "uint16"),
+    "ec": ("sbuf", [128, 2048], "bfloat16"), "em": ("sbuf", [128, 2048], "bfloat16"),
+    "ql0": ("sbuf", [128, 8], "uint16"), "ql1": ("sbuf", [128, 8], "uint16"),
+    "x0": ("sbuf", [128, 128], "bfloat16"), "x1": ("sbuf", [128, 128], "bfloat16"),
+    "y0": ("sbuf", [128, 128], "float16"), "y1": ("sbuf", [128, 128], "float16"), "yw0": ("sbuf", [128, 256], "float16"), "yw1": ("sbuf", [128, 256], "float16"),
+    "acc": ("sbuf", [128, 16], "float32"), "outb": ("sbuf", [128, 32], "float32"),
+    "kq": ("sbuf", [128, 9], "int32"), "kc": ("sbuf", [128, 9], "int32"), "kf": ("sbuf", [128, 9], "float32"),
+    "rm": ("sbuf", [128, 128], "bfloat16"), "rc": ("sbuf", [128, 128], "bfloat16"), "rg": ("sbuf", [128, 256], "bfloat16"), "rs": ("sbuf", [128, 128], "bfloat16"),
+    "one": ("sbuf", [128, 128], "bfloat16"), "sel": ("sbuf", [128, 128], "bfloat16"), "keep": ("sbuf", [128, 128], "bfloat16"),
+    "ro": ("sbuf", [128, 3], "float32"), "rb": ("sbuf", [128, 3], "float32"), "mv": ("sbuf", [128, 4], "float32"), "cf": ("sbuf", [128, 24], "float32"),
+    "gbd": ("sbuf", [128, 256], "bfloat16"), "d16": ("sbuf", [128, 16], "float32"), "b16": ("sbuf", [128, 16], "float32"),
+    "e16": ("sbuf", [128, 2048], "bfloat16"), "erw": ("sbuf", [128, 144], "bfloat16"), "pc": ("sbuf", [128, 16], "bfloat16"), "wc": ("sbuf", [128, 16], "bfloat16"),
+    "idh": ("sbuf", [128, 128], "float16"),
+    "la": ("sbuf", [128, 128], "bfloat16"), "lc": ("sbuf", [128, 128], "bfloat16"), "lb": ("sbuf", [128, 128], "bfloat16"), "li": ("sbuf", [128, 128], "bfloat16"),
+    "lbv": ("sbuf", [128, 512], "float16"), "liv": ("sbuf", [128, 512], "float16"),
+    "r2a": ("sbuf", [128, 128], "bfloat16"), "r2b": ("sbuf", [128, 128], "bfloat16"), "r2": ("sbuf", [128, 128], "bfloat16"), "r4": ("sbuf", [128, 128], "bfloat16"),
+}
+for _i in range(8):
+    SCRATCH["pb%d" % _i] = ("psum", [128, 512], "float32")
+SEMAPHORES = ["vv", "ss", "pp", "gq", "arrA", "arrE", "arrX", "arrO", "locA", "locE", "locX", "locO"] + ["d%d" % _i for _i in range(ND)]
+
+ADD, SUB, MUL, MAX, EQ = AluOpType.add, AluOpType.subtract, AluOpType.mult, AluOpType.max, AluOpType.is_equal
+AND, SHR = AluOpType.bitwise_and, AluOpType.logical_shift_right
+AF = ActivationFunctionType
+
+
+def rank_program(g, core, T, topo):
+    rank = T.rank_of(core)
+    if rank is None:
+        return
+    queues = {"v": g.vector, "s": g.scalar, "p": g.tensor, "g": g, "y": g.sync}
+    comp = {"v": "vv", "s": "ss", "p": "pp", "g": "gq"}
+    total, known, hist, bank, dmas = {}, {q: {} for q in queues}, {}, {}, [0]
+
+    def wait(q, tok):
+        sem, val, know = tok
+        if known[q].get(sem, 0) < val:
+            queues[q].wait_ge(T.sem[sem], val)
+            known[q][sem] = val
+            for a, b in know.items():
+                if known[q].get(a, 0) < b:
+                    known[q][a] = b
+
+    def deps(q, reads, writes, is_dma):
+        need = []
+        for regs, w in ((reads, False), (writes, True)):
+            for key, lo, hi in regs:
+                if key[:2] == "pb":
+                    for oq, tok in bank.get(key, {}).items():
+                        if oq != q:
+                            need.append(tok)
+                    continue
+                for l, h, tok, oq, ow in hist.get(key, []):
+                    if l < hi and lo < h and (w or ow):
+                        same = oq == q and not is_dma
+                        if same and w:
+                            continue
+                        need.append(tok)
+        best = {}
+        for tok in need:
+            if tok[0] not in best or best[tok[0]][1] < tok[1]:
+                best[tok[0]] = tok
+        toks = list(best.values())
+        for tok in toks:
+            if any(o is not tok and o[2].get(tok[0], 0) >= tok[1] for o in toks):
+                continue
+            wait(q, tok)
+
+    def note(q, tok, reads, writes, is_dma):
+        for regs, w in ((reads, False), (writes, True)):
+            for key, lo, hi in regs:
+                if key[:2] == "pb":
+                    bank.setdefault(key, {})[q] = tok
+                    continue
+                old = hist.setdefault(key, [])
+                if w:
+                    hist[key] = old = [o for o in old if not (lo <= o[0] and o[1] <= hi)]
+                old.append((lo, hi, tok, "dma" if is_dma else q, w))
+
+    def op(q, call, reads, writes):
+        deps(q, reads, writes, False)
+        sem = comp[q]
+        total[sem] = total.get(sem, 0) + 1
+        tok = (sem, total[sem], dict(known[q]))
+        call(queues[q]).then_inc(T.sem[sem], 1)
+        note(q, tok, reads, writes, False)
+        return tok
+
+    def dma(q, out, in_, reads, writes, extra=()):
+        for tok in extra:
+            wait(q, tok)
+        deps(q, reads, writes, True)
+        sem = "d%d" % dmas[0]
+        dmas[0] += 1
+        total[sem] = 16
+        tok = (sem, 16, dict(known[q]))
+        queues[q].dma_start(out, in_).then_inc(T.sem[sem], 16)
+        note(q, tok, reads, writes, True)
+        return tok
+
+    others = [s for s in range(4) if s != rank]
+    SHARE = 4
+
+    def send(src_of, dst, arr, loc, reads):
+        deps("g", reads, [], True)
+        tr = []
+        for i, s in enumerate(others):
+            dstc = T.cores[s]
+            a = topo.addr(dstc)
+            eng = topo.engines(core, dstc)[SHARE * i:SHARE * (i + 1)]
+            tr.append(RemoteDMATransfer(dst_ids=[DstId(rid=a[0], pnc=a[1])], dma_engine_mask=sum(1 << k for k in eng),
+                                        remote_sem=T.sem[arr], src=src_of(s), dst=dst))
+        g.remote_dma_fused(tr, local_sem=T.sem[loc])
+        total[loc] = 3 * SHARE
+        total[arr] = 3 * SHARE
+        return (arr, 3 * SHARE, {})
+
+    def ts(out, in0, s1, s2, *ops):
+        return lambda e: e.tensor_scalar(out, in0, s1, s2, *ops)
+
+    def tt(out, in0, in1, o):
+        return lambda e: e.tensor_tensor(out, in0, in1, o)
+
+    def cp(out, in_):
+        return lambda e: e.tensor_copy(out, in_)
+
+    def act(out, in_, func=AF.Copy, **kw):
+        return lambda e: e.activation(out, in_, func, **kw)
+
+    def mm(out, lhsT, rhs, start=True, stop=True):
+        return lambda e: e.matmul(out, lhsT, rhs, start, stop)
+
+    def iota(out, pattern, base=0):
+        return lambda e: e.iota(out, pattern, base, 0, allow_small_or_imprecise_dtypes=True)
+
+    def asel(out, in_, pattern, cmp_, fill, base):
+        return lambda e: e.affine_select(out, in_, pattern, cmp_, fill, base, 0)
+    W = 128
+
+    A3, E3, X3 = T.srcA, T.srcE, T.srcX
+    dma("y", A3[:, 0:64, :], T.nx[:], [], [("srcAn", 0, 1)])
+    dma("s", A3[:, 64:128, :], T.w[:], [], [("srcAw", 0, 1)])
+    dma("y", E3[:], T.e[:], [], [("srcE", 0, 1)])
+    dma("s", X3[:], T.x[:], [], [("srcX", 0, 1)])
+    own = slice(2 * rank, 2 * rank + 2)
+    rows = slice(32 * rank, 32 * rank + 32)
+    dma("y", T.landA[rank, 0:64, :], T.nx[own, :], [], [("landAn", 0, 1)])
+    dma("s", T.landA[rank, 64:128, :], T.w[own, :], [], [("landAw", 0, 1)])
+    dma("y", T.landE[rank], T.e[rows, :], [], [("landE", 0, 1)])
+    dma("s", T.landX[rank], T.x[rows, :], [], [("landX", 0, 1)])
+
+    op("g", lambda e: e.iota(T.kq[:], [[0, 9]], 0, 1), [], [("kq", 0, 9)])
+    op("g", iota(T.rm[:], [[1, 128]]), [], [("rm", 0, W)])
+    op("g", iota(T.rg[:], [[0, 2], [1, 8], [0, 16]]), [], [("rg", 0, 256)])
+    op("g", iota(T.rc[:], [[1, 32], [0, 4]]), [], [("rc", 0, W)])
+    arrA = send(lambda s: A3[s], T.landA[rank], "arrA", "locA", [("srcAn", 0, 1), ("srcAw", 0, 1)])
+    op("g", asel(T.rs[:], T.rc[:], [[0, 32], [1, 4]], AluOpType.is_gt, -1.0, 0), [("rc", 0, W)], [("rs", 0, W)])
+    op("g", iota(T.one[:], [[0, 128]], 1), [], [("one", 0, W)])
+    op("g", asel(T.sel[:], T.one[:], [[0, 32], [-1, 4]], AluOpType.is_gt, 0.0, 2), [("one", 0, W)], [("sel", 0, W)])
+    op("g", asel(T.keep[:], T.sel[:], [[0, 8], [1, 4], [0, 4]], AluOpType.not_equal, 1.0, -2), [("sel", 0, W)], [("keep", 0, W)])
+    arrE = send(lambda s: E3[s], T.landE[rank], "arrE", "locE", [("srcE", 0, 1)])
+    arrX = send(lambda s: X3[s], T.landX[rank], "arrX", "locX", [("srcX", 0, 1)])
+
+    kf, ro, rb, mv, cf = T.kf, T.ro, T.rb, T.mv, T.cf
+    for i, (o1, a1, o2, a2) in enumerate([(SHR, 4, None, 0), (AND, 15, None, 0), (AND, 3, None, 0), (SHR, 2, AND, 3),
+                                          (SHR, 5, None, 0), (SHR, 2, AND, 7), (AND, 1, None, 0), (SHR, 1, AND, 1), (AND, 127, None, 0)]):
+        c = ts(T.kc[:, i:i + 1], T.kq[:, i:i + 1], a1, None, o1) if o2 is None else ts(T.kc[:, i:i + 1], T.kq[:, i:i + 1], a1, a2, o1, o2)
+        op("v", c, [("kq", 0, 9)], [("kc", i, i + 1)])
+    op("v", cp(kf[:], T.kc[:]), [("kc", 0, 9)], [("kf", 0, 9)])
+    KF, RM, RC = ("kf", 0, 9), ("rm", 0, W), ("rc", 0, W)
+
+    def k(i):
+        return kf[:, i:i + 1]
+
+    def col(i):
+        return cf[:, i:i + 1]
+
+    def ck(i):
+        return ("cf", i, i + 1)
+
+    def cts(i, in0, s1, s2, ops, reads):
+        op("v", ts(col(i), in0, s1, s2, *ops), reads, [ck(i)])
+    for j in range(3):
+        op("v", ts(ro[:, j:j + 1], k(3), float(j), None, EQ), [KF], [("ro", j, j + 1)])
+    op("v", ts(T.d16[:], T.rm[:, 0:16], k(1), None, EQ), [RM, KF], [("d16", 0, 16)])
+    op("v", ts(T.b16[:], T.rm[:, 0:16], ro[:, 1:2], None, MUL), [RM, ("ro", 1, 2)], [("b16", 0, 16)])
+    op("v", ts(T.gbd[:], T.rg[:], k(0), None, EQ), [("rg", 0, 256), KF], [("gbd", 0, 256)])
+    for j in range(3):
+        op("v", ts(rb[:, j:j + 1], k(4), float(j), None, EQ), [KF], [("rb", j, j + 1)])
+    for j in range(4):
+        op("v", ts(mv[:, j:j + 1], k(2), float(j), None, EQ), [KF], [("mv", j, j + 1)])
+    cts(0, rb[:, 1:2], 0.0078125, rb[:, 0:1], (MUL, ADD), [("rb", 0, 2)])
+    cts(1, k(5), 4.0, k(4), (MUL, ADD), [KF])
+    cts(2, k(5), 4.0, 1.0, (MUL, ADD), [KF])
+    cts(3, rb[:, 0:1], -0.0078125, None, (MUL,), [("rb", 0, 1)])
+    cts(4, rb[:, 2:3], 1.0, col(0), (MUL, ADD), [("rb", 2, 3), ck(0)])
+    cts(5, ro[:, 1:2], 128.0, ro[:, 0:1], (MUL, ADD), [("ro", 0, 2)])
+    op("v", ts(T.lc[:], T.rc[:], col(2), col(3), EQ, MUL), [RC, ck(2), ck(3)], [("lc", 0, W)])
+    op("v", ts(T.la[:], T.rc[:], col(1), col(4), EQ, MUL), [RC, ck(1), ck(4)], [("la", 0, W)])
+    cts(6, k(2), 3.0, col(5), (EQ, MUL), [KF, ck(5)])
+    op("v", lambda e: e.memset(T.erw[:], 0.0), [], [("erw", 0, 144)])
+    op("v", tt(T.lb[:], T.la[:], T.lc[:], ADD), [("la", 0, W), ("lc", 0, W)], [("lb", 0, W)])
+    op("v", ts(T.idh[:], T.rm[:], k(8), None, EQ), [RM, KF], [("idh", 0, W)])
+    for v in range(4):
+        op("v", ts(T.lbv[:, W * v:W * v + W], T.lb[:], mv[:, v:v + 1], None, MUL), [("lb", 0, W), ("mv", v, v + 1)], [("lbv", W * v, W * v + W)])
+    op("v", ts(T.erw[:, 15:128:16], T.gbd[:, 0:128:16], col(6), None, MUL), [("gbd", 0, 256), ck(6)], [("erw", 0, 144)])
+    op("v", ts(T.pc[:], T.gbd[:, 0:256:16], col(5), None, MUL), [("gbd", 0, 256), ck(5)], [("pc", 0, 16)])
+    op("v", ts(T.wc[:], T.gbd[:, 0:256:16], ro[:, 2:3], None, MUL), [("gbd", 0, 256), ("ro", 2, 3)], [("wc", 0, 16)])
+    cts(7, k(6), 2.0, k(7), (MUL, ADD), [KF])
+    cts(8, k(0), 4.0, 7.0, (MUL, ADD), [KF])
+    cts(9, k(1), 10.0, None, (EQ,), [KF])
+    cts(10, k(1), 11.0, None, (EQ,), [KF])
+    cts(11, k(6), -1.0, 1.0, (MUL, ADD), [KF])
+    cts(12, k(8), 1.0, None, (ADD,), [KF])
+    cts(13, col(8), col(9), -5.0, (MUL, ADD), [ck(8), ck(9)])
+    cts(14, col(8), col(10), -5.0, (MUL, ADD), [ck(8), ck(10)])
+    cts(15, col(9), -1.0, col(11), (MUL, ADD), [ck(9), ck(11)])
+    cts(16, col(12), col(15), -1.0, (MUL, ADD), [ck(12), ck(15)])
+    op("v", ts(T.r4[:], T.rc[:], col(14), None, EQ), [RC, ck(14)], [("r4", 0, W)])
+    op("v", ts(T.r2a[:], T.rm[:], col(16), None, EQ), [RM, ck(16)], [("r2a", 0, W)])
+    op("v", ts(T.r2b[:], T.rs[:], col(13), None, EQ), [("rs", 0, W), ck(13)], [("r2b", 0, W)])
+    op("v", tt(T.r2[:], T.r2a[:], T.r2b[:], ADD), [("r2a", 0, W), ("r2b", 0, W)], [("r2", 0, W)])
+    op("v", tt(T.li[:], T.lb[:], T.keep[:], MUL), [("lb", 0, W), ("keep", 0, W)], [("li", 0, W)])
+    for v in range(4):
+        op("v", ts(T.liv[:, W * v:W * v + W], T.li[:], mv[:, v:v + 1], None, MUL), [("li", 0, W), ("mv", v, v + 1)], [("liv", W * v, W * v + W)])
+    for r in range(16):
+        op("s", act(T.tab[:, W * r:W * r + W], T.rm[:], AF.Identity, bias=T.b16[:, r:r + 1], scale=ro[:, 0:1]),
+           [RM, ("b16", 0, 16), ("ro", 0, 1)], [("tab", W * r, W * r + W)])
+    for r in range(16):
+        op("s", act(T.e16[:, W * r:W * r + W], T.gbd[:, 0:W], AF.Copy, scale=T.d16[:, r:r + 1]),
+           [("gbd", 0, 256), ("d16", 0, 16)], [("e16", W * r, W * r + W)])
+
+    nxl = T.landA[:, 0:64, :]
+    dma("y", T.s2r[0:32, :], nxl, [("landAn", 0, 1)], [("s2h", 0, 512)], [arrA])
+    dma("y", T.s2r[32:64, :], nxl, [("landAn", 0, 1)], [("s2l", 0, 512)], [arrA])
+    dma("y", T.s2r[64:96, :], T.landA[:, 64:128, :], [("landAw", 0, 1)], [("s2w", 0, 512)], [arrA])
+    for G in range(8):
+        q, y = G // 2, G % 2
+        dma("sy"[y], T.l1r[:, 16 * G:16 * G + 16], T.landA[q, 32 * y:32 * y + 32, :], [("landAn", 0, 1)], [("l1r", 16 * G, 16 * G + 16)], [arrA])
+    for t in range(4):
+        for r0, r1, sh in ((0, 4 - t, t), (4 - t, 4, t - 4)):
+            if r0 < r1:
+                dma("y", T.ep[32 * (r0 + sh):32 * (r1 + sh), :, 16 * t:16 * t + 16],
+                    T.landE[r0:r1, t // 2::2, 16 * (t % 2):16 * (t % 2) + 16], [("landE", 0, 1)], [("ep%d%d" % (t, r0), 0, 1)], [arrE])
+    dma("y", T.xr[:], T.landX[:], [("landX", 0, 1)], [("xr", 0, 16)], [arrX])
+    EPK = [("ep%d%d" % (t, r0), 0, 1) for t in range(4) for r0 in (0, 4 - t) if r0 < 4]
+
+    for h in range(2):
+        lo, hi = 256 * h, 256 * h + 256
+        op("v", ts(T.s2r[0:32, lo:hi], T.s2r[0:32, lo:hi], 127, None, AND), [("s2h", lo, hi)], [("s2h", lo, hi)])
+        op("v", cp(T.s2f[0:96, lo:hi], T.s2r[0:96, lo:hi]), [("s2h", lo, hi), ("s2l", lo, hi), ("s2w", lo, hi)], [("s2f", lo, hi)])
+        for v in range(4):
+            b = "pb%d" % (v + 4 * h)
+            op("p", mm(T[b][:, 0:256], T.lbv[0:96, W * v:W * v + W], T.s2f[0:96, lo:hi]),
+               [("lbv", W * v, W * v + W), ("s2f", lo, hi)], [(b, 0, 1)])
+
+    def copy0(q, v, h):
+        b, lo = "pb%d" % (v + 4 * h), 512 * v + 256 * h
+        c = act if q == "s" else cp
+        op(q, c(T.t0[:, lo:lo + 256], T[b][:, 0:256]), [(b, 0, 1)], [("t0", lo, lo + 256)])
+    for q, v, h in (("s", 0, 0), ("s", 1, 0), ("s", 2, 0), ("s", 3, 0), ("v", 0, 1)):
+        copy0(q, v, h)
+    op("v", cp(T.l1f[:], T.l1r[:]), [("l1r", 0, W)], [("l1f", 0, W)])
+    op("p", mm(T.pb0[:, 0:128], T.l1f[:], T.idh[:]), [("l1f", 0, W), ("idh", 0, W)], [("pb0", 0, 1)])
+    copy0("v", 1, 1)
+    copy0("s", 2, 1)
+    copy0("s", 3, 1)
+    op("v", cp(T.l1[:], T.pb0[:, 0:128]), [("pb0", 0, 1)], [("l1", 0, W)])
+    I1 = ["pb1", "pb2", "pb3", "pb0"]
+    for v in range(4):
+        op("p", mm(T[I1[v]][:], T.liv[0:96, W * v:W * v + W], T.s2f[0:96, :]),
+           [("liv", W * v, W * v + W), ("s2f", 0, 512)], [(I1[v], 0, 1)])
+
+    def gather(q, out, okey, lo, hi, win, wkey, w0, lst, lkey, mask=None):
+        src = win[:, w0:w0 + 2048].indirect(lst[:, lo // 16:hi // 16])
+        rd = [(wkey, w0, w0 + 2048), (lkey, lo // 16, hi // 16)]
+        if mask is not None:
+            rd.append(KF)
+        if q == "v":
+            op("v", cp(out[:, lo:hi], src) if mask is None else ts(out[:, lo:hi], src, mask, None, MUL), rd, [(okey, lo, hi)])
+        else:
+            op("s", act(out[:, lo:hi], src) if mask is None else act(out[:, lo:hi], src, scale=mask), rd, [(okey, lo, hi)])
+
+    def fix(dst, dkey, d0, buf, bkey, banks, lo, hi):
+        while lo < hi:
+            c = lo // 512
+            m = min(hi, 512 * c + 512)
+            op("v", tt(dst[:, d0 + lo:d0 + m], buf[:, lo:m], T[banks[c]][:, lo - 512 * c:m - 512 * c], MAX),
+               [(bkey, lo, m), (banks[c], 0, 1)], [(dkey, d0 + lo, d0 + m)])
+            lo = m
+
+    def relay(h, pbn, gbuf, gkey):
+        for r in range(16):
+            op("p", mm(T[pbn][:, 0:64], T.erw[:, 15 - r:143 - r], gbuf[:, 1024 * h + r:1024 * h + 1024:16], r == 0, r == 15),
+               [("erw", 0, 144), (gkey, 1024 * h, 1024 * h + 1024)], [(pbn, 0, 1)])
+
+    def relist(h, pbn, lst, lkey):
+        op("v", cp(lst[:, 64 * h:64 * h + 64], T[pbn][:, 0:64]), [(pbn, 0, 1)], [(lkey, 64 * h, 64 * h + 64)])
+
+    gather("v", T.ga, "ga", 0, 384, T.t0, "t0", 0, T.l1, "l1", k(7))
+    for lo, hi in ((384, 512), (512, 1024), (1024, 1536), (1536, 1888), (1888, 2048)):
+        gather("s", T.ga, "ga", lo, hi, T.t0, "t0", 0, T.l1, "l1", k(7))
+    relay(0, "pb4", T.ga, "ga")
+    fix(T.t1, "t1", 0, T.ga, "ga", I1, 0, 512)
+    fix(T.t1, "t1", 0, T.ga, "ga", I1, 512, 1024)
+    for l in range(2):
+        op("v", ts(T.ei[:, 64 * l:64 * l + 64], T.ep[:, l, :], 3, None, ADD), EPK, [("ei", 64 * l, 64 * l + 64)])
+    op("v", ts(T.fi[:], T.ei[:], 3, None, AND), [("ei", 0, W)], [("fi", 0, W)])
+    I2 = ["pb6", "pb7", "pb1", "pb2"]
+
+    def in2(c):
+        op("p", mm(T[I2[c]][:], T.r2[:], T.t1[:, 512 * c:512 * c + 512]), [("r2", 0, W), ("t1", 512 * c, 512 * c + 512)], [(I2[c], 0, 1)])
+    in2(0)
+    relay(1, "pb5", T.ga, "ga")
+    in2(1)
+    fix(T.t1, "t1", 0, T.ga, "ga", I1, 1024, 1536)
+    in2(2)
+    relist(0, "pb4", T.l2, "l2")
+    fix(T.t1, "t1", 0, T.ga, "ga", I1, 1536, 1888)
+    fix(T.t1, "t1", 0, T.ga, "ga", I1, 1888, 2048)
+    in2(3)
+
+    gather("v", T.gb, "gb", 0, 384, T.t1, "t1", 0, T.l2, "l2", k(6))
+    for lo, hi in ((384, 512), (512, 1024)):
+        gather("s", T.gb, "gb", lo, hi, T.t1, "t1", 0, T.l2, "l2", k(6))
+    relist(1, "pb5", T.l2, "l2")
+    fix(T.tab, "tab", 2048, T.gb, "gb", I2, 0, 512)
+    for lo, hi in ((1024, 1536), (1536, 1888), (1888, 2048)):
+        gather("s", T.gb, "gb", lo, hi, T.t1, "t1", 0, T.l2, "l2", k(6))
+    relay(0, "pb4", T.gb, "gb")
+    C4 = ["pb3", "pb0", "pb6", "pb7"]
+
+    def c4(c):
+        op("p", mm(T[C4[c]][:], T.r4[:], T.tab[:, 2048 + 512 * c:2560 + 512 * c]), [("r4", 0, W), ("tab", 2048 + 512 * c, 2560 + 512 * c)], [(C4[c], 0, 1)])
+    op("v", ts(T.ki[:], T.ei[:], 2, None, SHR), [("ei", 0, W)], [("ki", 0, W)])
+    fix(T.tab, "tab", 2048, T.gb, "gb", I2, 512, 1024)
+    op("v", cp(T.fb[:], T.fi[:]), [("fi", 0, W)], [("fb", 0, W)])
+    relay(1, "pb5", T.gb, "gb")
+    fix(T.tab, "tab", 2048, T.gb, "gb", I2, 1024, 1536)
+    fix(T.tab, "tab", 2048, T.gb, "gb", I2, 1536, 1888)
+    relist(0, "pb4", T.l4, "l4")
+    fix(T.tab, "tab", 2048, T.gb, "gb", I2, 1888, 2048)
+    for c in range(4):
+        c4(c)
+    N1, N2 = 576, 640
+    gather("v", T.ga, "ga", 0, 384, T.tab, "tab", 2048, T.l4, "l4")
+    gather("s", T.ga, "ga", N1, 1024, T.tab, "tab", 2048, T.l4, "l4")
+    relist(1, "pb5", T.l4, "l4")
+    gather("v", T.ga, "ga", 384, N1, T.tab, "tab", 2048, T.l4, "l4")
+    for lo, hi in ((1024, 1536), (1536, 1888), (1888, 2048)):
+        gather("s", T.ga, "ga", lo, hi, T.tab, "tab", 2048, T.l4, "l4")
+    EMB = ["pb1", "pb2", "pb4", "pb5"]
+    for c in range(4):
+        for r in range(16):
+            op("p", mm(T[EMB[c]][:, r:512:16], T.e16[:, W * r:W * r + W], T.fb[:, 32 * c:32 * c + 32]),
+               [("e16", W * r, W * r + W), ("fb", 32 * c, 32 * c + 32)], [(EMB[c], 0, 1)])
+    fix(T.tab, "tab", 4096, T.ga, "ga", C4, 0, 1024)
+    op("s", act(T.c4a[:, 0:512], T[C4[0]][:]), [(C4[0], 0, 1)], [("c4a", 0, 512)])
+    op("s", act(T.c4a[:, 512:N2], T[C4[1]][:, 0:N2 - 512]), [(C4[1], 0, 1)], [("c4a", 512, N2)])
+    for lo, hi in ((1024, 1536), (1536, 1888), (1888, 2048)):
+        fix(T.tab, "tab", 4096, T.ga, "ga", C4, lo, hi)
+
+    def ecopy(t):
+        lo = 256 * t
+        c = lo // 512
+        op("s", act(T.ec[:, lo:lo + 256], T[EMB[c]][:, lo - 512 * c:lo - 512 * c + 256]), [(EMB[c], 0, 1)], [("ec", lo, lo + 256)])
+
+    def emask(t):
+        lo = 256 * t
+        op("v", ts(T.em[:, lo:lo + 256], T.ec[:, lo:lo + 256], col(7), None, EQ), [("ec", lo, lo + 256), ck(7)], [("em", lo, lo + 256)])
+    for kk in (2, 3):
+        gbuf, gkey = (T.gb, "gb") if kk == 2 else (T.ga, "ga")
+        o = 2048 * kk + 2048
+        op("v", tt(T.tab[:, o:o + N2], T.tab[:, o - 2048:o].indirect(T.l4[:, 0:N2 // 16]), T.c4a[:, 0:N2], MAX),
+           [("tab", o - 2048, o), ("l4", 0, N2 // 16), ("c4a", 0, N2)], [("tab", o, o + N2)])
+        chunks = ((N2, 1024), (1024, 1536), (1536, 1888), (1888, 2048))
+        for lo, hi in chunks:
+            gather("s", gbuf, gkey, lo, hi, T.tab, "tab", o - 2048, T.l4, "l4")
+        if kk == 2:
+            ecopy(0)
+            ecopy(1)
+            op("v", ts(T.off[:], T.ki[:], 2048, None, MUL), [("ki", 0, W)], [("off", 0, W)])
+            op("v", tt(T.xe[:], T.xr[:], T.off[:, 0:16], ADD), [("xr", 0, 16), ("off", 0, 16)], [("xe", 0, 16)])
+            for b in range(2):
+                op("v", cp(T["ql%d" % b][:], T.xe[:, 8 * b:8 * b + 8]), [("xe", 0, 16)], [("ql%d" % b, 0, 8)])
+        for lo, hi in chunks:
+            fix(T.tab, "tab", o, gbuf, gkey, C4, lo, hi)
+            if kk == 3 and lo == 1024:
+                emask(0)
+    for t in range(2, 6):
+        ecopy(t)
+
+    PX, PL, PW, PLW = ["pb3", "pb0"], ["pb6", "pb7"], ["pb1", "pb2"], "pb4"
+
+    def look(t, b):
+        q, x = "ql%d" % b, "x%d" % b
+        lo = 256 * t + 128 * b
+        op("v", tt(T[x][:], T.tab[:].indirect(T[q][:]), T.em[:, lo:lo + 128], MUL), [("tab", 0, 10240), (q, 0, 8), ("em", lo, lo + 128)], [(x, 0, W)])
+
+    def sums(t, b):
+        x, y, yw, c, o = "x%d" % b, "y%d" % b, "yw%d" % b, 2 * (t % 4), W * (t % 2)
+        for r in range(16):
+            op("p", mm(T[PX[b]][0:8, r:128:16], T[x][:, r:128:16], T.pc[:, 6:14]), [(x, 0, W), ("pc", 0, 16)], [(PX[b], 0, 1)])
+        op("s", act(T[y][0:8, :], T[PX[b]][0:8, 0:128]), [(PX[b], 0, 1)], [(y, 0, W)])
+        for r in range(16):
+            op("p", mm(T[PW[b]][0:8, r:128:16], T[x][:, r:128:16], T.wc[:, c:c + 8]), [(x, 0, W), ("wc", 0, 16)], [(PW[b], 0, 1)])
+        op("s", act(T[yw][0:8, o:o + W], T[PW[b]][0:8, 0:128]), [(PW[b], 0, 1)], [(yw, o, o + W)])
+        if t < 7:
+            o = 16 * (t + 1) + 8 * b
+            op("p", mm(T[PL[b]][:, 0:8], T.idh[:], T.off[:, o:o + 8], True, False), [("idh", 0, W), ("off", o, o + 8)], [(PL[b], 0, 1)])
+
+    def turn(t, b):
+        y, q = "y%d" % b, "ql%d" % b
+        op("p", mm(T[PL[b]][:, 0:8], T[y][0:8, :], T.idh[0:8, 0:8], t == 7, True), [(y, 0, W), ("idh", 0, W)], [(PL[b], 0, 1)])
+        if t < 7:
+            op("v", cp(T[q][:], T[PL[b]][:, 0:8]), [(PL[b], 0, 1)], [(q, 0, 8)])
+        else:
+            op("v", cp(T.outb[:, 8 * b:8 * b + 8], T[PL[b]][:, 0:8]), [(PL[b], 0, 1)], [("outb", 8 * b, 8 * b + 8)])
+
+    def wturn(t, b):
+        yw, o = "yw%d" % b, W * (t % 2)
+        op("p", mm(T[PLW][:, 8 * b:8 * b + 8], T[yw][0:8, o:o + W], T.idh[0:8, 0:8]), [(yw, o, o + W), ("idh", 0, W)], [(PLW, 0, 1)])
+
+    def weigh(t):
+        if t == 0:
+            op("v", cp(T.acc[:], T[PLW][:, 0:16]), [(PLW, 0, 1)], [("acc", 0, 16)])
+        elif t < 7:
+            op("v", tt(T.acc[:], T.acc[:], T[PLW][:, 0:16], MAX), [(PLW, 0, 1), ("acc", 0, 16)], [("acc", 0, 16)])
+        else:
+            op("v", tt(T.outb[:, 16:32], T.acc[:], T[PLW][:, 0:16], MAX), [(PLW, 0, 1), ("acc", 0, 16)], [("outb", 16, 32)])
+
+    look(0, 0)
+    emask(1)
+    for t in range(8):
+        if t > 0:
+            turn(t - 1, 1)
+        sums(t, 0)
+        look(t, 1)
+        if t > 0:
+            wturn(t - 1, 0)
+            wturn(t - 1, 1)
+            weigh(t - 1)
+        if t == 1:
+            ecopy(6)
+            ecopy(7)
+        turn(t, 0)
+        sums(t, 1)
+        if t < 7:
+            look(t + 1, 0)
+        if t < 6:
+            emask(t + 2)
+    turn(7, 1)
+    wturn(7, 0)
+    wturn(7, 1)
+    weigh(7)
+
+    arrO = send(lambda s: T.outb[:], T.landO[rank], "arrO", "locO", [("outb", 0, 32)])
+    dma("y", T.landO[rank], T.outb[:], [("outb", 0, 32)], [("landO", 0, 1)])
+    dma("y", T.last[:], T.landO[:, rows, 0:16], [("landO", 0, 1)], [], [arrO])
+    dma("s", T.peak[:], T.landO[:, rows, 16:32], [("landO", 0, 1)], [], [arrO])
+    for sem, val in total.items():
+        if known["g"].get(sem, 0) < val:
+            g.wait_ge(T.sem[sem], val)

@@ -1,39 +1,38 @@
-import numpy as np
 from concourse.bass import DstId, RemoteDMATransfer
-from concourse.mybir import dt, AluOpType, ActivationFunctionType
+from concourse.mybir import AluOpType, ActivationFunctionType
 
 ND = 40
+M = 2048
+CUT = 1280
+RQ = "s"
 SCRATCH = {
-    "srcA": ("dram", [4, 128, 64], "int32"), "srcE": ("dram", [4, 128, 32], "int32"), "srcX": ("dram", [4, 128, 4], "int32"),
-    "landA": ("dram", [4, 128, 64], "int32"), "landE": ("dram", [4, 128, 32], "int32"), "landX": ("dram", [4, 128, 4], "int32"),
-    "landO": ("dram", [4, 128, 32], "float32"),
-    "s2r": ("sbuf", [128, 512], "int32"), "s2f": ("sbuf", [128, 512], "float16"), "l1r": ("sbuf", [128, 128], "int32"), "l1f": ("sbuf", [128, 128], "float16"),
-    "ep": ("sbuf", [128, 2, 64], "int32"), "ei": ("sbuf", [128, 128], "int32"), "fi": ("sbuf", [128, 128], "int32"), "ki": ("sbuf", [128, 128], "int32"),
-    "fb": ("sbuf", [128, 128], "bfloat16"), "off": ("sbuf", [128, 128], "float16"), "xr": ("sbuf", [128, 16], "int32"), "xe": ("sbuf", [128, 16], "int32"),
-    "t0": ("sbuf", [128, 2048], "bfloat16"), "t1": ("sbuf", [128, 2048], "bfloat16"), "tab": ("sbuf", [128, 10240], "bfloat16"),
-    "ga": ("sbuf", [128, 2048], "bfloat16"), "gb": ("sbuf", [128, 2048], "bfloat16"), "c4a": ("sbuf", [128, 640], "bfloat16"),
-    "l1": ("sbuf", [128, 128], "uint16"), "l2": ("sbuf", [128, 128], "uint16"), "l4": ("sbuf", [128, 128], "uint16"),
-    "ec": ("sbuf", [128, 2048], "bfloat16"), "em": ("sbuf", [128, 2048], "bfloat16"),
-    "ql0": ("sbuf", [128, 8], "uint16"), "ql1": ("sbuf", [128, 8], "uint16"),
-    "x0": ("sbuf", [128, 128], "bfloat16"), "x1": ("sbuf", [128, 128], "bfloat16"),
-    "y0": ("sbuf", [128, 128], "float16"), "y1": ("sbuf", [128, 128], "float16"), "yw0": ("sbuf", [128, 256], "float16"), "yw1": ("sbuf", [128, 256], "float16"),
-    "acc": ("sbuf", [128, 16], "float32"), "outb": ("sbuf", [128, 32], "float32"),
-    "kq": ("sbuf", [128, 9], "int32"), "kc": ("sbuf", [128, 9], "int32"), "kf": ("sbuf", [128, 9], "float32"),
-    "rm": ("sbuf", [128, 128], "bfloat16"), "rc": ("sbuf", [128, 128], "bfloat16"), "rg": ("sbuf", [128, 256], "bfloat16"), "rs": ("sbuf", [128, 128], "bfloat16"),
-    "one": ("sbuf", [128, 128], "bfloat16"), "sel": ("sbuf", [128, 128], "bfloat16"), "keep": ("sbuf", [128, 128], "bfloat16"),
-    "ro": ("sbuf", [128, 3], "float32"), "rb": ("sbuf", [128, 3], "float32"), "mv": ("sbuf", [128, 4], "float32"), "cf": ("sbuf", [128, 24], "float32"),
-    "gbd": ("sbuf", [128, 256], "bfloat16"), "d16": ("sbuf", [128, 16], "float32"), "b16": ("sbuf", [128, 16], "float32"),
-    "e16": ("sbuf", [128, 2048], "bfloat16"), "erw": ("sbuf", [128, 144], "bfloat16"), "pc": ("sbuf", [128, 16], "bfloat16"), "wc": ("sbuf", [128, 16], "bfloat16"),
-    "idh": ("sbuf", [128, 128], "float16"),
-    "la": ("sbuf", [128, 128], "bfloat16"), "lc": ("sbuf", [128, 128], "bfloat16"), "lb": ("sbuf", [128, 128], "bfloat16"), "li": ("sbuf", [128, 128], "bfloat16"),
-    "lbv": ("sbuf", [128, 512], "float16"), "liv": ("sbuf", [128, 512], "float16"),
-    "r2a": ("sbuf", [128, 128], "bfloat16"), "r2b": ("sbuf", [128, 128], "bfloat16"), "r2": ("sbuf", [128, 128], "bfloat16"), "r4": ("sbuf", [128, 128], "bfloat16"),
+    "srcA": ("dram", [4, 128, 64], "int32"), "srcE": ("dram", [4, 128, 48], "uint16"),
+    "landA": ("dram", [4, 128, 64], "int32"), "landE": ("dram", [4, 128, 48], "uint16"), "landO": ("dram", [4, 128, 32], "float32"),
+    "er": ("sbuf", [128, 4, 32], "int32"), "xr": ("sbuf", [128, 16], "int32"), "ed": ("sbuf", [128, 4, 32], "bfloat16"),
+    "et": ("sbuf", [128, 4, 32], "bfloat16"), "es": ("sbuf", [128, 4, 16], "bfloat16"), "eu": ("sbuf", [128, 4, 48], "uint16"),
+    "xo": ("sbuf", [128, 16], "float32"), "xs": ("sbuf", [128, 16], "float32"),
+    "r0": ("sbuf", [128, M], "int32"), "s2r": ("sbuf", [128, 512], "int32"), "s2f": ("sbuf", [128, 512], "float16"),
+    "l1r": ("sbuf", [128, 128], "int32"), "l1f": ("sbuf", [128, 128], "float16"),
+    "t1": ("sbuf", [128, M], "float32"), "t2": ("sbuf", [128, M], "float32"), "tab": ("sbuf", [128, 3 * M], "float32"),
+    "ga": ("sbuf", [128, M], "float16"), "gb": ("sbuf", [128, M], "float16"), "gc": ("sbuf", [128, M], "float16"),
+    "l1": ("sbuf", [128, 128], "uint16"), "l2": ("sbuf", [128, 128], "uint16"), "l4": ("sbuf", [128, 128], "uint16"), "l8": ("sbuf", [128, 128], "uint16"),
+    "ep": ("sbuf", [128, 2, 64], "uint16"), "off": ("sbuf", [128, 2, 64], "float16"), "em": ("sbuf", [128, M], "bfloat16"),
+    "ql0": ("sbuf", [128, 16], "uint16"), "ql1": ("sbuf", [128, 16], "uint16"),
+    "x0": ("sbuf", [128, 256], "float16"), "x1": ("sbuf", [128, 256], "float16"),
+    "z0": ("sbuf", [128, 256], "float16"), "z1": ("sbuf", [128, 256], "float16"),
+    "pk": ("sbuf", [128, 256], "float16"), "yw": ("sbuf", [128, 128], "float16"), "outb": ("sbuf", [128, 32], "float32"),
+    "kq": ("sbuf", [128, 10], "int32"), "kc": ("sbuf", [128, 10], "int32"), "kf": ("sbuf", [128, 10], "float32"), "cf": ("sbuf", [128, 40], "float32"),
+    "rm": ("sbuf", [128, 144], "bfloat16"), "r64": ("sbuf", [128, 128], "bfloat16"), "r16": ("sbuf", [128, 128], "bfloat16"), "r8": ("sbuf", [128, 16], "bfloat16"),
+    "idh": ("sbuf", [128, 128], "float16"), "lb": ("sbuf", [128, 128], "float16"), "lbv": ("sbuf", [128, 512], "float16"),
+    "mg": ("sbuf", [128, 384], "float16"), "rw": ("sbuf", [128, 576], "float16"), "sw": ("sbuf", [128, 128], "float16"),
+    "pm": ("sbuf", [128, 512], "float16"), "seg": ("sbuf", [128, 256], "bfloat16"), "mtab": ("sbuf", [128, 16], "bfloat16"),
 }
 for _i in range(8):
     SCRATCH["pb%d" % _i] = ("psum", [128, 512], "float32")
-SEMAPHORES = ["vv", "ss", "pp", "gq", "arrA", "arrE", "arrX", "arrO", "locA", "locE", "locX", "locO"] + ["d%d" % _i for _i in range(ND)]
+SEMAPHORES = ["vv", "ss", "pp", "gq", "arrA", "arrE", "arrO", "locA", "locE", "locO"] + ["d%d" % _i for _i in range(ND)]
 
-ADD, SUB, MUL, MAX, EQ = AluOpType.add, AluOpType.subtract, AluOpType.mult, AluOpType.max, AluOpType.is_equal
+ADD, MUL, MAX, MIN = AluOpType.add, AluOpType.mult, AluOpType.max, AluOpType.min
+EQ, GE, GT, LT = AluOpType.is_equal, AluOpType.is_ge, AluOpType.is_gt, AluOpType.is_lt
 AND, SHR = AluOpType.bitwise_and, AluOpType.logical_shift_right
 AF = ActivationFunctionType
 
@@ -67,7 +66,7 @@ def rank_program(g, core, T, topo):
                 for l, h, tok, oq, ow in hist.get(key, []):
                     if l < hi and lo < h and (w or ow):
                         same = oq == q and not is_dma
-                        if same and w:
+                        if same and w and not ow:
                             continue
                         need.append(tok)
         best = {}
@@ -91,7 +90,9 @@ def rank_program(g, core, T, topo):
                     hist[key] = old = [o for o in old if not (lo <= o[0] and o[1] <= hi)]
                 old.append((lo, hi, tok, "dma" if is_dma else q, w))
 
-    def op(q, call, reads, writes):
+    def op(q, call, reads, writes, extra=()):
+        for tok in extra:
+            wait(q, tok)
         deps(q, reads, writes, False)
         sem = comp[q]
         total[sem] = total.get(sem, 0) + 1
@@ -138,340 +139,326 @@ def rank_program(g, core, T, topo):
     def cp(out, in_):
         return lambda e: e.tensor_copy(out, in_)
 
-    def act(out, in_, func=AF.Copy, **kw):
-        return lambda e: e.activation(out, in_, func, **kw)
+    def act(out, in_):
+        return lambda e: e.activation(out, in_, AF.Copy)
+
+    def move(q, out, in_):
+        return act(out, in_) if q == "s" else cp(out, in_)
+
+    def fill(out, c):
+        return lambda e: e.memset(out, c)
 
     def mm(out, lhsT, rhs, start=True, stop=True):
         return lambda e: e.matmul(out, lhsT, rhs, start, stop)
 
-    def iota(out, pattern, base=0):
-        return lambda e: e.iota(out, pattern, base, 0, allow_small_or_imprecise_dtypes=True)
+    def iota(out, pattern, base=0, cm=0):
+        return lambda e: e.iota(out, pattern, base, cm, allow_small_or_imprecise_dtypes=True)
 
-    def asel(out, in_, pattern, cmp_, fill, base):
-        return lambda e: e.affine_select(out, in_, pattern, cmp_, fill, base, 0)
+    def all_(name):
+        return (name, 0, 1 << 20)
     W = 128
 
-    A3, E3, X3 = T.srcA, T.srcE, T.srcX
-    dma("y", A3[:, 0:64, :], T.nx[:], [], [("srcAn", 0, 1)])
-    dma("s", A3[:, 64:128, :], T.w[:], [], [("srcAw", 0, 1)])
-    dma("y", E3[:], T.e[:], [], [("srcE", 0, 1)])
-    dma("s", X3[:], T.x[:], [], [("srcX", 0, 1)])
+    A3 = T.srcA
     own = slice(2 * rank, 2 * rank + 2)
     rows = slice(32 * rank, 32 * rank + 32)
-    dma("y", T.landA[rank, 0:64, :], T.nx[own, :], [], [("landAn", 0, 1)])
-    dma("s", T.landA[rank, 64:128, :], T.w[own, :], [], [("landAw", 0, 1)])
-    dma("y", T.landE[rank], T.e[rows, :], [], [("landE", 0, 1)])
-    dma("s", T.landX[rank], T.x[rows, :], [], [("landX", 0, 1)])
+    dma("y", A3[:, 0:64, :], T.nx[:], [], [all_("srcAn")])
+    dma("s", A3[:, 64:128, :], T.w[:], [], [all_("srcAw")])
+    dma("y", T.er[:], T.e[:], [], [all_("er")])
+    dma("s", T.xr[:], T.x[:], [], [all_("xr")])
+    dma("y", T.landA[rank, 0:64, :], T.nx[own, :], [], [all_("landAn")])
+    dma("s", T.landA[rank, 64:128, :], T.w[own, :], [], [all_("landAw")])
 
-    op("g", lambda e: e.iota(T.kq[:], [[0, 9]], 0, 1), [], [("kq", 0, 9)])
-    op("g", iota(T.rm[:], [[1, 128]]), [], [("rm", 0, W)])
-    op("g", iota(T.rg[:], [[0, 2], [1, 8], [0, 16]]), [], [("rg", 0, 256)])
-    op("g", iota(T.rc[:], [[1, 32], [0, 4]]), [], [("rc", 0, W)])
-    arrA = send(lambda s: A3[s], T.landA[rank], "arrA", "locA", [("srcAn", 0, 1), ("srcAw", 0, 1)])
-    op("g", asel(T.rs[:], T.rc[:], [[0, 32], [1, 4]], AluOpType.is_gt, -1.0, 0), [("rc", 0, W)], [("rs", 0, W)])
-    op("g", iota(T.one[:], [[0, 128]], 1), [], [("one", 0, W)])
-    op("g", asel(T.sel[:], T.one[:], [[0, 32], [-1, 4]], AluOpType.is_gt, 0.0, 2), [("one", 0, W)], [("sel", 0, W)])
-    op("g", asel(T.keep[:], T.sel[:], [[0, 8], [1, 4], [0, 4]], AluOpType.not_equal, 1.0, -2), [("sel", 0, W)], [("keep", 0, W)])
-    arrE = send(lambda s: E3[s], T.landE[rank], "arrE", "locE", [("srcE", 0, 1)])
-    arrX = send(lambda s: X3[s], T.landX[rank], "arrX", "locX", [("srcX", 0, 1)])
+    op("g", lambda e: e.iota(T.kq[:], [[0, 10]], 0, 1), [], [all_("kq")])
+    op("g", iota(T.rm[:], [[1, 144]]), [], [all_("rm")])
+    op("g", iota(T.r16[:], [[0, 8], [1, 16]]), [], [all_("r16")])
+    op("g", iota(T.r64[:], [[0, 2], [1, 64]]), [], [all_("r64")])
+    tok = op("g", iota(T.r8[:], [[0, 2], [1, 8]]), [], [all_("r8")])
+    arrA = send(lambda s: A3[s], T.landA[rank], "arrA", "locA", [all_("srcAn"), all_("srcAw")])
+    tokp = op("g", lambda e: e.iota(T.s2r[64:96, :], [[1, 512]], 0, 512), [], [all_("s2i")], [tok])
 
-    kf, ro, rb, mv, cf = T.kf, T.ro, T.rb, T.mv, T.cf
-    for i, (o1, a1, o2, a2) in enumerate([(SHR, 4, None, 0), (AND, 15, None, 0), (AND, 3, None, 0), (SHR, 2, AND, 3),
-                                          (SHR, 5, None, 0), (SHR, 2, AND, 7), (AND, 1, None, 0), (SHR, 1, AND, 1), (AND, 127, None, 0)]):
-        c = ts(T.kc[:, i:i + 1], T.kq[:, i:i + 1], a1, None, o1) if o2 is None else ts(T.kc[:, i:i + 1], T.kq[:, i:i + 1], a1, a2, o1, o2)
-        op("v", c, [("kq", 0, 9)], [("kc", i, i + 1)])
-    op("v", cp(kf[:], T.kc[:]), [("kc", 0, 9)], [("kf", 0, 9)])
-    KF, RM, RC = ("kf", 0, 9), ("rm", 0, W), ("rc", 0, W)
+    op("v", fill(T.r0[:], 0), [], [all_("r0n"), all_("r0w")])
+    kf, cf = T.kf, T.cf
+    PF = [(AND, 127), (AND, 15), (AND, 112), (AND, 3), (SHR, 4, AND, 1), (SHR, 4), (AND, 7), (SHR, 3, AND, 1), (SHR, 2, AND, 1), (SHR, 6)]
+    for i, f in enumerate(PF):
+        kc, kq = T.kc[:, i:i + 1], T.kq[:, i:i + 1]
+        op("v", ts(kc, kq, f[1], None, f[0]) if len(f) == 2 else ts(kc, kq, f[1], f[3], f[0], f[2]), [all_("kq")], [("kc", i, i + 1)])
+    op("v", cp(kf[:], T.kc[:]), [all_("kc")], [all_("kf")])
+    KF, RM = all_("kf"), all_("rm")
+    names = {}
 
     def k(i):
         return kf[:, i:i + 1]
 
-    def col(i):
-        return cf[:, i:i + 1]
+    def col(n):
+        return cf[:, names[n]:names[n] + 1]
 
-    def ck(i):
-        return ("cf", i, i + 1)
+    def ck(n):
+        return ("cf", names[n], names[n] + 1)
 
-    def cts(i, in0, s1, s2, ops, reads):
-        op("v", ts(col(i), in0, s1, s2, *ops), reads, [ck(i)])
-    for j in range(3):
-        op("v", ts(ro[:, j:j + 1], k(3), float(j), None, EQ), [KF], [("ro", j, j + 1)])
-    op("v", ts(T.d16[:], T.rm[:, 0:16], k(1), None, EQ), [RM, KF], [("d16", 0, 16)])
-    op("v", ts(T.b16[:], T.rm[:, 0:16], ro[:, 1:2], None, MUL), [RM, ("ro", 1, 2)], [("b16", 0, 16)])
-    op("v", ts(T.gbd[:], T.rg[:], k(0), None, EQ), [("rg", 0, 256), KF], [("gbd", 0, 256)])
-    for j in range(3):
-        op("v", ts(rb[:, j:j + 1], k(4), float(j), None, EQ), [KF], [("rb", j, j + 1)])
-    for j in range(4):
-        op("v", ts(mv[:, j:j + 1], k(2), float(j), None, EQ), [KF], [("mv", j, j + 1)])
-    cts(0, rb[:, 1:2], 0.0078125, rb[:, 0:1], (MUL, ADD), [("rb", 0, 2)])
-    cts(1, k(5), 4.0, k(4), (MUL, ADD), [KF])
-    cts(2, k(5), 4.0, 1.0, (MUL, ADD), [KF])
-    cts(3, rb[:, 0:1], -0.0078125, None, (MUL,), [("rb", 0, 1)])
-    cts(4, rb[:, 2:3], 1.0, col(0), (MUL, ADD), [("rb", 2, 3), ck(0)])
-    cts(5, ro[:, 1:2], 128.0, ro[:, 0:1], (MUL, ADD), [("ro", 0, 2)])
-    op("v", ts(T.lc[:], T.rc[:], col(2), col(3), EQ, MUL), [RC, ck(2), ck(3)], [("lc", 0, W)])
-    op("v", ts(T.la[:], T.rc[:], col(1), col(4), EQ, MUL), [RC, ck(1), ck(4)], [("la", 0, W)])
-    cts(6, k(2), 3.0, col(5), (EQ, MUL), [KF, ck(5)])
-    op("v", lambda e: e.memset(T.erw[:], 0.0), [], [("erw", 0, 144)])
-    op("v", tt(T.lb[:], T.la[:], T.lc[:], ADD), [("la", 0, W), ("lc", 0, W)], [("lb", 0, W)])
-    op("v", ts(T.idh[:], T.rm[:], k(8), None, EQ), [RM, KF], [("idh", 0, W)])
+    def cts(n, in0, s1, s2, *ops):
+        def val(a):
+            if isinstance(a, str):
+                return k(int(a[1:])) if a[1:].isdigit() else col(a)
+            return a
+        rd = [KF] + [ck(a) for a in (in0, s1, s2) if isinstance(a, str) and not a[1:].isdigit()]
+        args = (val(in0), val(s1), val(s2))
+        names[n] = len(names)
+        op("v", ts(col(n), args[0], args[1], args[2], *ops), rd, [ck(n)])
+
+    def match(out, okey, row, rkey, at, on=None):
+        rd = [rkey, KF] + [ck(a) for a in (at, on) if a in names]
+        a = col(at) if at in names else k(int(at[1:]))
+        if on is None:
+            op("v", ts(out, row, a, None, EQ), rd, [okey])
+        else:
+            op("v", ts(out, row, a, col(on) if on in names else k(int(on[1:])), EQ, MUL), rd, [okey])
+
+    cts("y0", "k4", -1.0, 1.0, MUL, ADD)
+    op("v", fill(T.eu[:], 0), [], [all_("eu")])
+    op("v", ts(T.ed[:, :, 0:16], T.er[:, :, 16:32], col("y0"), None, MUL), [all_("er"), ck("y0")], [("ed", 0, 1)])
+    op("v", ts(T.ed[:, :, 16:32], T.er[:, :, 16:32], k(4), None, MUL), [all_("er"), KF], [("ed", 1, 2)])
+    op("v", ts(T.xo[:], T.er[:, 0, 0:16], 8, M, GE, MUL), [all_("er")], [all_("xo")])
+    op("v", cp(T.eu[:, :, 0:16], T.er[:, :, 0:16]), [all_("er")], [("eu", 0, 1)])
+    op("v", lambda e: e.transpose(T.et[:], T.ed[:]), [all_("ed")], [all_("et")])
+    op("v", tt(T.xs[:], T.xo[:], T.xr[:], ADD), [all_("xo"), all_("xr")], [all_("xs")])
+    op("v", tt(T.es[:], T.et[:, :, 0:16], T.et[:, :, 16:32], ADD), [all_("et")], [all_("es")])
+    op("v", cp(T.eu[:, 0, 32:48], T.xs[:]), [all_("xs")], [("eu", 1, 2)])
+    op("v", cp(T.eu[:, :, 16:32], T.es[:]), [all_("es")], [("eu", 2, 3)])
+    dma("y", T.srcE[:], T.eu[:], [all_("eu")], [all_("srcE")])
+    dma("s", T.landE[rank], T.eu[rows, :, :], [all_("eu")], [all_("landE")])
+    arrE = send(lambda s: T.srcE[s], T.landE[rank], "arrE", "locE", [all_("srcE")])
+    op("g", iota(T.tab[:, 0:M], [[0, M]]), [], [("tab", 0, M)], [tokp])
+
+    match(T.idh[:], all_("idh"), T.rm[:, 0:W], RM, "k0")
+    cts("la", "k5", 32.0, 1.0, MUL, ADD)
+    cts("lb", "k8", 16.0, "la", MUL, ADD)
+    cts("lc", "k7", 7.0, "lb", MUL, ADD)
+    op("v", ts(T.lb[0:64, :], T.rm[0:64, 0:W], cf[0:64, names["lc"]:names["lc"] + 1], None, EQ), [RM, ck("lc")], [("lb", 0, 1)])
+    op("v", ts(T.lb[64:128, :], T.r16[64:128, :], 0.0, None, EQ), [all_("r16")], [("lb", 1, 2)])
     for v in range(4):
-        op("v", ts(T.lbv[:, W * v:W * v + W], T.lb[:], mv[:, v:v + 1], None, MUL), [("lb", 0, W), ("mv", v, v + 1)], [("lbv", W * v, W * v + W)])
-    op("v", ts(T.erw[:, 15:128:16], T.gbd[:, 0:128:16], col(6), None, MUL), [("gbd", 0, 256), ck(6)], [("erw", 0, 144)])
-    op("v", ts(T.pc[:], T.gbd[:, 0:256:16], col(5), None, MUL), [("gbd", 0, 256), ck(5)], [("pc", 0, 16)])
-    op("v", ts(T.wc[:], T.gbd[:, 0:256:16], ro[:, 2:3], None, MUL), [("gbd", 0, 256), ("ro", 2, 3)], [("wc", 0, 16)])
-    cts(7, k(6), 2.0, k(7), (MUL, ADD), [KF])
-    cts(8, k(0), 4.0, 7.0, (MUL, ADD), [KF])
-    cts(9, k(1), 10.0, None, (EQ,), [KF])
-    cts(10, k(1), 11.0, None, (EQ,), [KF])
-    cts(11, k(6), -1.0, 1.0, (MUL, ADD), [KF])
-    cts(12, k(8), 1.0, None, (ADD,), [KF])
-    cts(13, col(8), col(9), -5.0, (MUL, ADD), [ck(8), ck(9)])
-    cts(14, col(8), col(10), -5.0, (MUL, ADD), [ck(8), ck(10)])
-    cts(15, col(9), -1.0, col(11), (MUL, ADD), [ck(9), ck(11)])
-    cts(16, col(12), col(15), -1.0, (MUL, ADD), [ck(12), ck(15)])
-    op("v", ts(T.r4[:], T.rc[:], col(14), None, EQ), [RC, ck(14)], [("r4", 0, W)])
-    op("v", ts(T.r2a[:], T.rm[:], col(16), None, EQ), [RM, ck(16)], [("r2a", 0, W)])
-    op("v", ts(T.r2b[:], T.rs[:], col(13), None, EQ), [("rs", 0, W), ck(13)], [("r2b", 0, W)])
-    op("v", tt(T.r2[:], T.r2a[:], T.r2b[:], ADD), [("r2a", 0, W), ("r2b", 0, W)], [("r2", 0, W)])
-    op("v", tt(T.li[:], T.lb[:], T.keep[:], MUL), [("lb", 0, W), ("keep", 0, W)], [("li", 0, W)])
+        cts("v%d_" % v, "k3", float(v), None, EQ)
     for v in range(4):
-        op("v", ts(T.liv[:, W * v:W * v + W], T.li[:], mv[:, v:v + 1], None, MUL), [("li", 0, W), ("mv", v, v + 1)], [("liv", W * v, W * v + W)])
-    for r in range(16):
-        op("s", act(T.tab[:, W * r:W * r + W], T.rm[:], AF.Identity, bias=T.b16[:, r:r + 1], scale=ro[:, 0:1]),
-           [RM, ("b16", 0, 16), ("ro", 0, 1)], [("tab", W * r, W * r + W)])
-    for r in range(16):
-        op("s", act(T.e16[:, W * r:W * r + W], T.gbd[:, 0:W], AF.Copy, scale=T.d16[:, r:r + 1]),
-           [("gbd", 0, 256), ("d16", 0, 16)], [("e16", W * r, W * r + W)])
+        op("v", ts(T.lbv[:, W * v:W * v + W], T.lb[:], col("v%d_" % v), None, MUL), [all_("lb"), ck("v%d_" % v)], [("lbv", W * v, W * v + W)])
+    cts("ja", "k7", -7.5, "k1", MUL, ADD)
+    cts("jb", "k1", 0.0, 100.0, EQ, MUL)
+    cts("jc", "ja", "jb", None, ADD)
+    cts("c15", "k2", 15.0, None, ADD)
+    STEP = ((1, 1.0), (2, 2.0), (4, 3.5))
+    for i, (s, thr) in enumerate(STEP):
+        cts("ma%d_" % i, "jc", thr, -1000.0, GT, MUL)
+        cts("ra%d_" % i, "k1", float(s), None, EQ)
+    for i, (s, thr) in enumerate(STEP):
+        cts("mb%d_" % i, "ma%d_" % i, "k0", float(s), ADD, ADD)
+        match(T.rw[:, 144 * i:144 * i + 144], ("rw", i, i + 1), T.rm[:], RM, "c15", "ra%d_" % i)
+    for i in range(3):
+        match(T.mg[:, W * i:W * i + W], ("mg", i, i + 1), T.rm[:, 0:W], RM, "mb%d_" % i)
+    cts("lo8", "k7", -1.0, 1.0, MUL, ADD)
+    cts("na", "k2", 96.0, -128.0, GE, MUL)
+    cts("nb", "na", "k2", 47.0, ADD, ADD)
+    cts("sa", "k5", 8.0, "k6", MUL, ADD)
+    cts("pa", "k6", 16.0, "k5", MUL, ADD)
+    cts("pb", "pa", 8.0, None, ADD)
+    cts("ta", "k6", "k7", None, ADD)
+    cts("tb", "lo8", 100.0, "ta", MUL, ADD)
+    match(T.rw[:, 432:576], ("rw", 3, 4), T.rm[:], RM, "nb", "lo8")
+    match(T.sw[:], all_("sw"), T.r64[:], all_("r64"), "sa", "k7")
+    for h in range(2):
+        for h2 in range(2):
+            i = 2 * h + h2
+            match(T.pm[:, W * i:W * i + W], ("pm", i, i + 1), T.rm[:, 0:W], RM, ("pa", "pb")[h], ("lo8", "k7")[h2])
+    op("v", ts(T.mtab[:], T.r8[:], col("tb"), col("ta"), MIN, EQ), [all_("r8"), ck("ta"), ck("tb")], [all_("mtab")])
+    op("v", fill(T.seg[:], 1.0), [], [all_("seg")])
+    op("v", fill(T.seg[:, 0:256:16], 0.0), [], [all_("seg")])
 
-    nxl = T.landA[:, 0:64, :]
-    dma("y", T.s2r[0:32, :], nxl, [("landAn", 0, 1)], [("s2h", 0, 512)], [arrA])
-    dma("y", T.s2r[32:64, :], nxl, [("landAn", 0, 1)], [("s2l", 0, 512)], [arrA])
-    dma("y", T.s2r[64:96, :], T.landA[:, 64:128, :], [("landAw", 0, 1)], [("s2w", 0, 512)], [arrA])
+    LA = [all_("landAn"), all_("landAw")]
     for G in range(8):
         q, y = G // 2, G % 2
-        dma("sy"[y], T.l1r[:, 16 * G:16 * G + 16], T.landA[q, 32 * y:32 * y + 32, :], [("landAn", 0, 1)], [("l1r", 16 * G, 16 * G + 16)], [arrA])
+        dma("sy"[y], T.l1r[:, 16 * G:16 * G + 16], T.landA[q, 32 * y:32 * y + 32, :], LA[:1], [("l1r", 16 * G, 16 * G + 16)], [arrA])
+    dma("y", T.r0[1:128:16, :], T.landA[:, 0:64, :], LA[:1], [all_("r0n")], [arrA])
+    dma("s", T.r0[8:128:16, :], T.landA[:, 64:128, :], LA[1:], [all_("r0w")], [arrA])
+    dma("y", T.s2r[0:64, :], T.landA[:], LA, [all_("s2m")], [arrA])
     for t in range(4):
         for r0, r1, sh in ((0, 4 - t, t), (4 - t, 4, t - 4)):
             if r0 < r1:
                 dma("y", T.ep[32 * (r0 + sh):32 * (r1 + sh), :, 16 * t:16 * t + 16],
-                    T.landE[r0:r1, t // 2::2, 16 * (t % 2):16 * (t % 2) + 16], [("landE", 0, 1)], [("ep%d%d" % (t, r0), 0, 1)], [arrE])
-    dma("y", T.xr[:], T.landX[:], [("landX", 0, 1)], [("xr", 0, 16)], [arrX])
-    EPK = [("ep%d%d" % (t, r0), 0, 1) for t in range(4) for r0 in (0, 4 - t) if r0 < 4]
+                    T.landE[r0:r1, t // 2::2, 16 * (t % 2):16 * (t % 2) + 16], [all_("landE")], [("ep", 2 * t + (r0 > 0), 2 * t + (r0 > 0) + 1)], [arrE])
+    dma("y", T.ql0[:], T.landE[:, 0::4, 32:48], [all_("landE")], [all_("ql0")], [arrE])
 
-    for h in range(2):
-        lo, hi = 256 * h, 256 * h + 256
-        op("v", ts(T.s2r[0:32, lo:hi], T.s2r[0:32, lo:hi], 127, None, AND), [("s2h", lo, hi)], [("s2h", lo, hi)])
-        op("v", cp(T.s2f[0:96, lo:hi], T.s2r[0:96, lo:hi]), [("s2h", lo, hi), ("s2l", lo, hi), ("s2w", lo, hi)], [("s2f", lo, hi)])
-        for v in range(4):
-            b = "pb%d" % (v + 4 * h)
-            op("p", mm(T[b][:, 0:256], T.lbv[0:96, W * v:W * v + W], T.s2f[0:96, lo:hi]),
-               [("lbv", W * v, W * v + W), ("s2f", lo, hi)], [(b, 0, 1)])
+    op("v", cp(T.l1f[:], T.l1r[:]), [all_("l1r")], [all_("l1f")])
+    op("p", mm(T.pb6[:, 0:W], T.l1f[:], T.idh[:]), [all_("l1f"), all_("idh")], [("pb6", 0, 1)])
+    op("v", cp(T.l1[:], T.pb6[:, 0:W]), [("pb6", 0, 1)], [all_("l1")])
+    op("s", act(T.s2f[0:96, :], T.s2r[0:96, :]), [all_("s2m"), all_("s2i")], [all_("s2f")])
+    TB = ["pb0", "pb1", "pb2", "pb3"]
 
-    def copy0(q, v, h):
-        b, lo = "pb%d" % (v + 4 * h), 512 * v + 256 * h
-        c = act if q == "s" else cp
-        op(q, c(T.t0[:, lo:lo + 256], T[b][:, 0:256]), [(b, 0, 1)], [("t0", lo, lo + 256)])
-    for q, v, h in (("s", 0, 0), ("s", 1, 0), ("s", 2, 0), ("s", 3, 0), ("v", 0, 1)):
-        copy0(q, v, h)
-    op("v", cp(T.l1f[:], T.l1r[:]), [("l1r", 0, W)], [("l1f", 0, W)])
-    op("p", mm(T.pb0[:, 0:128], T.l1f[:], T.idh[:]), [("l1f", 0, W), ("idh", 0, W)], [("pb0", 0, 1)])
-    copy0("v", 1, 1)
-    copy0("s", 2, 1)
-    copy0("s", 3, 1)
-    op("v", cp(T.l1[:], T.pb0[:, 0:128]), [("pb0", 0, 1)], [("l1", 0, W)])
-    I1 = ["pb1", "pb2", "pb3", "pb0"]
-    for v in range(4):
-        op("p", mm(T[I1[v]][:], T.liv[0:96, W * v:W * v + W], T.s2f[0:96, :]),
-           [("liv", W * v, W * v + W), ("s2f", 0, 512)], [(I1[v], 0, 1)])
+    def first(c):
+        op("p", mm(T[TB[c]][:], T.lbv[0:68, W * c:W * c + W], T.s2f[0:68, :], True, False),
+           [("lbv", W * c, W * c + W), all_("s2f")], [(TB[c], 0, 1)])
+    for c in range(4):
+        first(c)
 
-    def gather(q, out, okey, lo, hi, win, wkey, w0, lst, lkey, mask=None):
-        src = win[:, w0:w0 + 2048].indirect(lst[:, lo // 16:hi // 16])
-        rd = [(wkey, w0, w0 + 2048), (lkey, lo // 16, hi // 16)]
-        if mask is not None:
-            rd.append(KF)
-        if q == "v":
-            op("v", cp(out[:, lo:hi], src) if mask is None else ts(out[:, lo:hi], src, mask, None, MUL), rd, [(okey, lo, hi)])
-        else:
-            op("s", act(out[:, lo:hi], src) if mask is None else act(out[:, lo:hi], src, scale=mask), rd, [(okey, lo, hi)])
+    def gather(q, out, okey, o0, lo, hi, win, wkeys, lst):
+        op(q, move(q, out[:, o0 + lo:o0 + hi], win.indirect(T[lst][:, lo // 16:hi // 16])),
+           wkeys + [(lst, lo // 16, hi // 16)], [(okey, o0 + lo, o0 + hi)])
 
-    def fix(dst, dkey, d0, buf, bkey, banks, lo, hi):
-        while lo < hi:
+    def relist(h, lst, q="v"):
+        b = "pb%d" % (4 + h)
+        op(q, move(q, T[lst][:, 64 * h:64 * h + 64], T[b][:, 0:64]), [(b, 0, 1)], [(lst, 64 * h, 64 * h + 64)])
+
+    GK = ["ga", "gb", "gc"]
+
+    def level(i, win, wkeys, lst, dst, d0, nxt):
+        gk = GK[i]
+
+        def piece(q, lo, hi):
+            gather(q, T[gk], gk, 0, lo, hi, win, wkeys, lst)
+
+        def merge(lo, hi, start, j=i):
             c = lo // 512
-            m = min(hi, 512 * c + 512)
-            op("v", tt(dst[:, d0 + lo:d0 + m], buf[:, lo:m], T[banks[c]][:, lo - 512 * c:m - 512 * c], MAX),
-               [(bkey, lo, m), (banks[c], 0, 1)], [(dkey, d0 + lo, d0 + m)])
-            lo = m
+            op("p", mm(T[TB[c]][:, lo - 512 * c:hi - 512 * c], T.mg[:, W * j:W * j + W], T[GK[j]][:, lo:hi], start, j == i),
+               [("mg", j, j + 1), (GK[j], lo, hi)], [(TB[c], 0, 1)])
 
-    def relay(h, pbn, gbuf, gkey):
-        for r in range(16):
-            op("p", mm(T[pbn][:, 0:64], T.erw[:, 15 - r:143 - r], gbuf[:, 1024 * h + r:1024 * h + 1024:16], r == 0, r == 15),
-               [("erw", 0, 144), (gkey, 1024 * h, 1024 * h + 1024)], [(pbn, 0, 1)])
+        def relay(h, r0=0, r1=16):
+            b = "pb%d" % (4 + h)
+            for r in range(r0, r1):
+                op("p", mm(T[b][:, 0:64], T.rw[:, 144 * i + 15 - r:144 * i + 143 - r], T[gk][:, 1024 * h + r:1024 * h + 1024:16], r == 0, r == 15),
+                   [("rw", i, i + 1), (gk, 1024 * h, 1024 * h + 1024)], [(b, 0, 1)])
 
-    def relist(h, pbn, lst, lkey):
-        op("v", cp(lst[:, 64 * h:64 * h + 64], T[pbn][:, 0:64]), [(pbn, 0, 1)], [(lkey, 64 * h, 64 * h + 64)])
+        def out(q, lo, hi, add=False):
+            c = lo // 512
+            src = T[TB[c]][:, lo - 512 * c:hi - 512 * c]
+            if add:
+                op("v", tt(T[dst][:, d0 + lo:d0 + hi], T[wkeys[0][0]][:, lo:hi], src, ADD), [(TB[c], 0, 1)] + wkeys, [(dst, d0 + lo, d0 + hi)])
+            else:
+                op(q, move(q, T[dst][:, d0 + lo:d0 + hi], src), [(TB[c], 0, 1)], [(dst, d0 + lo, d0 + hi)])
+        if i == 0:
+            for q, lo in (("v", 0), ("s", 512), ("v", 1024), ("s", 1536)):
+                piece(q, lo, lo + 512)
+            merge(0, 512, False)
+            merge(512, 1024, False)
+            relay(0, 0, 8)
+            merge(1024, 1536, False)
+            merge(1536, M, False)
+            relay(0, 8, 16)
+            out("v", 0, 512)
+            out("s", 512, 1024)
+            out("v", 1024, 1536)
+            out("s", 1536, M)
+            relist(0, nxt)
+            relay(1)
+            return
+        piece("v", 0, 256)
+        piece("s", 512, 1024)
+        relist(1, lst)
+        piece("v", 256, 512)
+        piece("v", 1024, CUT)
+        piece("s", 1536, M)
+        piece("s", CUT, 1536)
+        first(1)
+        for j in range(i):
+            merge(512, 1024, False, j)
+        merge(0, 512, True)
+        merge(512, 1024, False)
+        merge(1024, CUT, True)
+        out("v", 0, 512, True)
+        out("v", 1024, CUT, True)
+        relay(0, 0, 6)
+        merge(1536, M, True)
+        relay(0, 6, 16)
+        merge(CUT, 1536, True)
+        out("s", 512, 1024)
+        out("v", 1536, M, True)
+        relist(0, nxt, RQ)
+        out("v", CUT, 1536, True)
+        relay(1)
 
-    gather("v", T.ga, "ga", 0, 384, T.t0, "t0", 0, T.l1, "l1", k(7))
-    for lo, hi in ((384, 512), (512, 1024), (1024, 1536), (1536, 1888), (1888, 2048)):
-        gather("s", T.ga, "ga", lo, hi, T.t0, "t0", 0, T.l1, "l1", k(7))
-    relay(0, "pb4", T.ga, "ga")
-    fix(T.t1, "t1", 0, T.ga, "ga", I1, 0, 512)
-    fix(T.t1, "t1", 0, T.ga, "ga", I1, 512, 1024)
-    for l in range(2):
-        op("v", ts(T.ei[:, 64 * l:64 * l + 64], T.ep[:, l, :], 3, None, ADD), EPK, [("ei", 64 * l, 64 * l + 64)])
-    op("v", ts(T.fi[:], T.ei[:], 3, None, AND), [("ei", 0, W)], [("fi", 0, W)])
-    I2 = ["pb6", "pb7", "pb1", "pb2"]
+    level(0, T.r0[:], [all_("r0n"), all_("r0w")], "l1", "t1", 0, "l2")
+    level(1, T.t1[:], [all_("t1")], "l2", "t2", 0, "l4")
+    level(2, T.t2[:], [all_("t2")], "l4", "tab", M, "l8")
 
-    def in2(c):
-        op("p", mm(T[I2[c]][:], T.r2[:], T.t1[:, 512 * c:512 * c + 512]), [("r2", 0, W), ("t1", 512 * c, 512 * c + 512)], [(I2[c], 0, 1)])
-    in2(0)
-    relay(1, "pb5", T.ga, "ga")
-    in2(1)
-    fix(T.t1, "t1", 0, T.ga, "ga", I1, 1024, 1536)
-    in2(2)
-    relist(0, "pb4", T.l2, "l2")
-    fix(T.t1, "t1", 0, T.ga, "ga", I1, 1536, 1888)
-    fix(T.t1, "t1", 0, T.ga, "ga", I1, 1888, 2048)
-    in2(3)
+    def elist(t):
+        return T.ep[:, t // 4, 16 * (t % 4):16 * (t % 4) + 16]
 
-    gather("v", T.gb, "gb", 0, 384, T.t1, "t1", 0, T.l2, "l2", k(6))
-    for lo, hi in ((384, 512), (512, 1024)):
-        gather("s", T.gb, "gb", lo, hi, T.t1, "t1", 0, T.l2, "l2", k(6))
-    relist(1, "pb5", T.l2, "l2")
-    fix(T.tab, "tab", 2048, T.gb, "gb", I2, 0, 512)
-    for lo, hi in ((1024, 1536), (1536, 1888), (1888, 2048)):
-        gather("s", T.gb, "gb", lo, hi, T.t1, "t1", 0, T.l2, "l2", k(6))
-    relay(0, "pb4", T.gb, "gb")
-    C4 = ["pb3", "pb0", "pb6", "pb7"]
+    def mask(t):
+        op("s", act(T.em[:, 256 * t:256 * t + 256], T.mtab[:].indirect(elist(t))), [all_("mtab"), all_("ep")], [("em", 256 * t, 256 * t + 256)])
+    A, AK = T.tab[:, M:2 * M], [("tab", M, 2 * M)]
+    NV = 1184
+    gather("v", T.tab, "tab", 2 * M, 0, 256, A, AK, "l8")
+    gather("s", T.tab, "tab", 2 * M, 512, 1024, A, AK, "l8")
+    relist(1, "l8")
+    gather("v", T.tab, "tab", 2 * M, 256, 512, A, AK, "l8")
+    op("v", ts(T.off[:], T.ep[:], 8, M, GE, MUL), [all_("ep")], [all_("off")])
+    gather("v", T.tab, "tab", 2 * M, 1024, 512 + NV, A, AK, "l8")
+    gather("s", T.tab, "tab", 2 * M, 512 + NV, M, A, AK, "l8")
+    mask(0)
 
-    def c4(c):
-        op("p", mm(T[C4[c]][:], T.r4[:], T.tab[:, 2048 + 512 * c:2560 + 512 * c]), [("r4", 0, W), ("tab", 2048 + 512 * c, 2560 + 512 * c)], [(C4[c], 0, 1)])
-    op("v", ts(T.ki[:], T.ei[:], 2, None, SHR), [("ei", 0, W)], [("ki", 0, W)])
-    fix(T.tab, "tab", 2048, T.gb, "gb", I2, 512, 1024)
-    op("v", cp(T.fb[:], T.fi[:]), [("fi", 0, W)], [("fb", 0, W)])
-    relay(1, "pb5", T.gb, "gb")
-    fix(T.tab, "tab", 2048, T.gb, "gb", I2, 1024, 1536)
-    fix(T.tab, "tab", 2048, T.gb, "gb", I2, 1536, 1888)
-    relist(0, "pb4", T.l4, "l4")
-    fix(T.tab, "tab", 2048, T.gb, "gb", I2, 1888, 2048)
-    for c in range(4):
-        c4(c)
-    N1, N2 = 576, 640
-    gather("v", T.ga, "ga", 0, 384, T.tab, "tab", 2048, T.l4, "l4")
-    gather("s", T.ga, "ga", N1, 1024, T.tab, "tab", 2048, T.l4, "l4")
-    relist(1, "pb5", T.l4, "l4")
-    gather("v", T.ga, "ga", 384, N1, T.tab, "tab", 2048, T.l4, "l4")
-    for lo, hi in ((1024, 1536), (1536, 1888), (1888, 2048)):
-        gather("s", T.ga, "ga", lo, hi, T.tab, "tab", 2048, T.l4, "l4")
-    EMB = ["pb1", "pb2", "pb4", "pb5"]
-    for c in range(4):
-        for r in range(16):
-            op("p", mm(T[EMB[c]][:, r:512:16], T.e16[:, W * r:W * r + W], T.fb[:, 32 * c:32 * c + 32]),
-               [("e16", W * r, W * r + W), ("fb", 32 * c, 32 * c + 32)], [(EMB[c], 0, 1)])
-    fix(T.tab, "tab", 4096, T.ga, "ga", C4, 0, 1024)
-    op("s", act(T.c4a[:, 0:512], T[C4[0]][:]), [(C4[0], 0, 1)], [("c4a", 0, 512)])
-    op("s", act(T.c4a[:, 512:N2], T[C4[1]][:, 0:N2 - 512]), [(C4[1], 0, 1)], [("c4a", 512, N2)])
-    for lo, hi in ((1024, 1536), (1536, 1888), (1888, 2048)):
-        fix(T.tab, "tab", 4096, T.ga, "ga", C4, lo, hi)
+    PL, PW = ["pb4", "pb5"], ["pb6", "pb7"]
 
-    def ecopy(t):
-        lo = 256 * t
-        c = lo // 512
-        op("s", act(T.ec[:, lo:lo + 256], T[EMB[c]][:, lo - 512 * c:lo - 512 * c + 256]), [(EMB[c], 0, 1)], [("ec", lo, lo + 256)])
+    def look(t, h):
+        q, x, lo = "ql%d" % (t % 2), "x%d" % (t % 2), 256 * t + W * h
+        op("v", tt(T[x][:, W * h:W * h + W], T.tab[:, M:3 * M].indirect(T[q][:, 8 * h:8 * h + 8]), T.em[:, lo:lo + W], MUL),
+           [("tab", M, 3 * M), all_(q), ("em", lo, lo + W)], [(x, W * h, W * h + W)])
 
-    def emask(t):
-        lo = 256 * t
-        op("v", ts(T.em[:, lo:lo + 256], T.ec[:, lo:lo + 256], col(7), None, EQ), [("ec", lo, lo + 256), ck(7)], [("em", lo, lo + 256)])
-    for kk in (2, 3):
-        gbuf, gkey = (T.gb, "gb") if kk == 2 else (T.ga, "ga")
-        o = 2048 * kk + 2048
-        op("v", tt(T.tab[:, o:o + N2], T.tab[:, o - 2048:o].indirect(T.l4[:, 0:N2 // 16]), T.c4a[:, 0:N2], MAX),
-           [("tab", o - 2048, o), ("l4", 0, N2 // 16), ("c4a", 0, N2)], [("tab", o, o + N2)])
-        chunks = ((N2, 1024), (1024, 1536), (1536, 1888), (1888, 2048))
-        for lo, hi in chunks:
-            gather("s", gbuf, gkey, lo, hi, T.tab, "tab", o - 2048, T.l4, "l4")
-        if kk == 2:
-            ecopy(0)
-            ecopy(1)
-            op("v", ts(T.off[:], T.ki[:], 2048, None, MUL), [("ki", 0, W)], [("off", 0, W)])
-            op("v", tt(T.xe[:], T.xr[:], T.off[:, 0:16], ADD), [("xr", 0, 16), ("off", 0, 16)], [("xe", 0, 16)])
-            for b in range(2):
-                op("v", cp(T["ql%d" % b][:], T.xe[:, 8 * b:8 * b + 8]), [("xe", 0, 16)], [("ql%d" % b, 0, 8)])
-        for lo, hi in chunks:
-            fix(T.tab, "tab", o, gbuf, gkey, C4, lo, hi)
-            if kk == 3 and lo == 1024:
-                emask(0)
-    for t in range(2, 6):
-        ecopy(t)
+    def early(t):
+        q, z = "ql%d" % (t % 2), "z%d" % (t % 2)
+        op("s", act(T[z][:], T.tab[:, 0:2 * M].indirect(T[q][:])), [("tab", 0, 2 * M), all_(q)], [all_(z)])
 
-    PX, PL, PW, PLW = ["pb3", "pb0"], ["pb6", "pb7"], ["pb1", "pb2"], "pb4"
+    def places(t, h):
+        x, b = "x%d" % (t % 2), PL[t % 2]
+        if h == 0 and t < 7:
+            n = t + 1
+            op("p", mm(T[b][:, 0:16], T.idh[:], T.off[:, n // 4, 16 * (n % 4):16 * (n % 4) + 16], True, False), [all_("idh"), all_("off")], [(b, 0, 1)])
+        for a in range(8 * h, 8 * h + 8):
+            op("p", mm(T[b][:, 0:16], T.rw[:, 447 - a:575 - a], T[x][:, 16 * a:16 * a + 16], t == 7 and a == 0, a == 15),
+               [("rw", 3, 4), (x, W * h, W * h + W)], [(b, 0, 1)])
 
-    def look(t, b):
-        q, x = "ql%d" % b, "x%d" % b
-        lo = 256 * t + 128 * b
-        op("v", tt(T[x][:], T.tab[:].indirect(T[q][:]), T.em[:, lo:lo + 128], MUL), [("tab", 0, 10240), (q, 0, 8), ("em", lo, lo + 128)], [(x, 0, W)])
+    def weights(t):
+        x, z, b, c = "x%d" % (t % 2), "z%d" % (t % 2), PW[t % 2], 16 * (t % 4)
+        sel = T.sw[:, c:c + 64]
+        for h in range(2):
+            o = W * h
+            op("p", mm(T[b][:, o + 1:o + W:2], T[z][:, o:o + W], sel), [all_(z), all_("sw")], [(b, 0, 1)])
+        for h in range(2):
+            o = W * h
+            op("p", mm(T[b][:, o:o + W:2], T[x][:, o:o + W], sel, True, t == 0), [(x, o, o + W), all_("sw")], [(b, 0, 1)])
+            if t > 0:
+                for h0 in range(2):
+                    i = 2 * h0 + h
+                    op("p", mm(T[b][:, o + 14:o + W:16], T.pm[:, W * i:W * i + W], T.pk[:, W * h0 + 15:W * h0 + W:16], False, h0 == 1),
+                       [("pm", i, i + 1), all_("pk")], [(b, 0, 1)])
 
-    def sums(t, b):
-        x, y, yw, c, o = "x%d" % b, "y%d" % b, "yw%d" % b, 2 * (t % 4), W * (t % 2)
-        for r in range(16):
-            op("p", mm(T[PX[b]][0:8, r:128:16], T[x][:, r:128:16], T.pc[:, 6:14]), [(x, 0, W), ("pc", 0, 16)], [(PX[b], 0, 1)])
-        op("s", act(T[y][0:8, :], T[PX[b]][0:8, 0:128]), [(PX[b], 0, 1)], [(y, 0, W)])
-        for r in range(16):
-            op("p", mm(T[PW[b]][0:8, r:128:16], T[x][:, r:128:16], T.wc[:, c:c + 8]), [(x, 0, W), ("wc", 0, 16)], [(PW[b], 0, 1)])
-        op("s", act(T[yw][0:8, o:o + W], T[PW[b]][0:8, 0:128]), [(PW[b], 0, 1)], [(yw, o, o + W)])
-        if t < 7:
-            o = 16 * (t + 1) + 8 * b
-            op("p", mm(T[PL[b]][:, 0:8], T.idh[:], T.off[:, o:o + 8], True, False), [("idh", 0, W), ("off", o, o + 8)], [(PL[b], 0, 1)])
+    def scan(t):
+        b = PW[t % 2]
+        op("v", lambda e: e.tensor_tensor_scan(T.pk[:], T.seg[:], T[b][:, 0:256], 0.0, MUL, MAX), [all_("seg"), (b, 0, 1)], [all_("pk")])
 
-    def turn(t, b):
-        y, q = "y%d" % b, "ql%d" % b
-        op("p", mm(T[PL[b]][:, 0:8], T[y][0:8, :], T.idh[0:8, 0:8], t == 7, True), [(y, 0, W), ("idh", 0, W)], [(PL[b], 0, 1)])
-        if t < 7:
-            op("v", cp(T[q][:], T[PL[b]][:, 0:8]), [(PL[b], 0, 1)], [(q, 0, 8)])
-        else:
-            op("v", cp(T.outb[:, 8 * b:8 * b + 8], T[PL[b]][:, 0:8]), [(PL[b], 0, 1)], [("outb", 8 * b, 8 * b + 8)])
-
-    def wturn(t, b):
-        yw, o = "yw%d" % b, W * (t % 2)
-        op("p", mm(T[PLW][:, 8 * b:8 * b + 8], T[yw][0:8, o:o + W], T.idh[0:8, 0:8]), [(yw, o, o + W), ("idh", 0, W)], [(PLW, 0, 1)])
-
-    def weigh(t):
-        if t == 0:
-            op("v", cp(T.acc[:], T[PLW][:, 0:16]), [(PLW, 0, 1)], [("acc", 0, 16)])
-        elif t < 7:
-            op("v", tt(T.acc[:], T.acc[:], T[PLW][:, 0:16], MAX), [(PLW, 0, 1), ("acc", 0, 16)], [("acc", 0, 16)])
-        else:
-            op("v", tt(T.outb[:, 16:32], T.acc[:], T[PLW][:, 0:16], MAX), [(PLW, 0, 1), ("acc", 0, 16)], [("outb", 16, 32)])
-
-    look(0, 0)
-    emask(1)
     for t in range(8):
-        if t > 0:
-            turn(t - 1, 1)
-        sums(t, 0)
+        look(t, 0)
+        early(t)
+        places(t, 0)
         look(t, 1)
-        if t > 0:
-            wturn(t - 1, 0)
-            wturn(t - 1, 1)
-            weigh(t - 1)
-        if t == 1:
-            ecopy(6)
-            ecopy(7)
-        turn(t, 0)
-        sums(t, 1)
+        places(t, 1)
         if t < 7:
-            look(t + 1, 0)
-        if t < 6:
-            emask(t + 2)
-    turn(7, 1)
-    wturn(7, 0)
-    wturn(7, 1)
-    weigh(7)
+            mask(t + 1)
+        if t > 0:
+            scan(t - 1)
+        weights(t)
+        b = PL[t % 2]
+        if t < 7:
+            q = "ql%d" % ((t + 1) % 2)
+            op("v", cp(T[q][:], T[b][:, 0:16]), [(b, 0, 1)], [all_(q)])
+        else:
+            op("s", act(T.outb[:, 0:16], T[b][:, 0:16]), [(b, 0, 1)], [("outb", 0, 16)])
+    scan(7)
+    for h in range(2):
+        for r in range(8):
+            op("p", mm(T.pb0[0:16, 8 * h + r:W:16], T.idh[:, 16 * r:16 * r + 16], T.pk[:, W * h + 15:W * h + W:16]), [all_("idh"), all_("pk")], [("pb0", 0, 1)])
+    op("v", cp(T.yw[0:16, :], T.pb0[0:16, 0:W]), [("pb0", 0, 1)], [all_("yw")])
+    op("p", mm(T.pb1[:, 0:16], T.yw[0:16, :], T.idh[0:16, 0:16]), [all_("yw"), all_("idh")], [("pb1", 0, 1)])
+    op("v", cp(T.outb[:, 16:32], T.pb1[:, 0:16]), [("pb1", 0, 1)], [("outb", 16, 32)])
 
-    arrO = send(lambda s: T.outb[:], T.landO[rank], "arrO", "locO", [("outb", 0, 32)])
-    dma("y", T.landO[rank], T.outb[:], [("outb", 0, 32)], [("landO", 0, 1)])
-    dma("y", T.last[:], T.landO[:, rows, 0:16], [("landO", 0, 1)], [], [arrO])
-    dma("s", T.peak[:], T.landO[:, rows, 16:32], [("landO", 0, 1)], [], [arrO])
+    arrO = send(lambda s: T.outb[:], T.landO[rank], "arrO", "locO", [all_("outb")])
+    dma("y", T.landO[rank], T.outb[:], [all_("outb")], [all_("landO")])
+    dma("y", T.last[:], T.landO[:, rows, 0:16], [all_("landO")], [], [arrO])
+    dma("s", T.peak[:], T.landO[:, rows, 16:32], [all_("landO")], [], [arrO])
     for sem, val in total.items():
         if known["g"].get(sem, 0) < val:
             g.wait_ge(T.sem[sem], val)

@@ -3,16 +3,15 @@ from concourse.mybir import AluOpType, ActivationFunctionType
 
 ND = 40
 M = 2048
-CUT = 1280
-RQ = "s"
+CUT, C2, R0, R1 = 1280, 1696, 4, 10
 SCRATCH = {
     "srcA": ("dram", [4, 128, 64], "int32"), "srcE": ("dram", [4, 128, 48], "uint16"),
     "landA": ("dram", [4, 128, 64], "int32"), "landE": ("dram", [4, 128, 48], "uint16"), "landO": ("dram", [4, 128, 32], "float32"),
     "er": ("sbuf", [128, 4, 32], "int32"), "xr": ("sbuf", [128, 16], "int32"), "ed": ("sbuf", [128, 4, 32], "bfloat16"),
     "et": ("sbuf", [128, 4, 32], "bfloat16"), "es": ("sbuf", [128, 4, 16], "bfloat16"), "eu": ("sbuf", [128, 4, 48], "uint16"),
     "xo": ("sbuf", [128, 16], "float32"), "xs": ("sbuf", [128, 16], "float32"),
-    "r0": ("sbuf", [128, M], "int32"), "s2r": ("sbuf", [128, 512], "int32"), "s2f": ("sbuf", [128, 512], "float16"),
-    "l1r": ("sbuf", [128, 128], "int32"), "l1f": ("sbuf", [128, 128], "float16"),
+    "r0": ("sbuf", [128, M], "int32"), "k0": ("sbuf", [128, 512], "float16"),
+    "l1r": ("sbuf", [128, 128], "int32"), "l1h": ("sbuf", [128, 128], "float16"), "l1f": ("sbuf", [128, 128], "float16"),
     "t1": ("sbuf", [128, M], "float32"), "t2": ("sbuf", [128, M], "float32"), "tab": ("sbuf", [128, 3 * M], "float32"),
     "ga": ("sbuf", [128, M], "float16"), "gb": ("sbuf", [128, M], "float16"), "gc": ("sbuf", [128, M], "float16"),
     "l1": ("sbuf", [128, 128], "uint16"), "l2": ("sbuf", [128, 128], "uint16"), "l4": ("sbuf", [128, 128], "uint16"), "l8": ("sbuf", [128, 128], "uint16"),
@@ -20,19 +19,20 @@ SCRATCH = {
     "ql0": ("sbuf", [128, 16], "uint16"), "ql1": ("sbuf", [128, 16], "uint16"),
     "x0": ("sbuf", [128, 256], "float16"), "x1": ("sbuf", [128, 256], "float16"),
     "z0": ("sbuf", [128, 256], "float16"), "z1": ("sbuf", [128, 256], "float16"),
-    "pk": ("sbuf", [128, 256], "float16"), "yw": ("sbuf", [128, 128], "float16"), "outb": ("sbuf", [128, 32], "float32"),
-    "kq": ("sbuf", [128, 10], "int32"), "kc": ("sbuf", [128, 10], "int32"), "kf": ("sbuf", [128, 10], "float32"), "cf": ("sbuf", [128, 40], "float32"),
-    "rm": ("sbuf", [128, 144], "bfloat16"), "r64": ("sbuf", [128, 128], "bfloat16"), "r16": ("sbuf", [128, 128], "bfloat16"), "r8": ("sbuf", [128, 16], "bfloat16"),
-    "idh": ("sbuf", [128, 128], "float16"), "lb": ("sbuf", [128, 128], "float16"), "lbv": ("sbuf", [128, 512], "float16"),
+    "pk": ("sbuf", [128, 256], "float16"), "pk7": ("sbuf", [128, 256], "float16"),
+    "yw": ("sbuf", [128, 128], "float16"), "y6": ("sbuf", [128, 128], "float16"), "outb": ("sbuf", [128, 32], "float32"),
+    "kq": ("sbuf", [128, 8], "int32"), "kc": ("sbuf", [128, 8], "int32"), "kf": ("sbuf", [128, 8], "float32"), "cf": ("sbuf", [128, 40], "float32"),
+    "rm": ("sbuf", [128, 144], "bfloat16"), "r64": ("sbuf", [128, 128], "bfloat16"), "r8": ("sbuf", [128, 16], "bfloat16"),
+    "b16": ("sbuf", [128, 16], "float32"), "idh": ("sbuf", [128, 128], "float16"),
     "mg": ("sbuf", [128, 384], "float16"), "rw": ("sbuf", [128, 576], "float16"), "sw": ("sbuf", [128, 128], "float16"),
     "pm": ("sbuf", [128, 512], "float16"), "seg": ("sbuf", [128, 256], "bfloat16"), "mtab": ("sbuf", [128, 16], "bfloat16"),
 }
 for _i in range(8):
     SCRATCH["pb%d" % _i] = ("psum", [128, 512], "float32")
-SEMAPHORES = ["vv", "ss", "pp", "gq", "arrA", "arrE", "arrO", "locA", "locE", "locO"] + ["d%d" % _i for _i in range(ND)]
+SEMAPHORES = ["vv", "ss", "pp", "gq", "arrA", "arrL", "arrE", "arrO", "locA", "locL", "locE", "locO"] + ["d%d" % _i for _i in range(ND)]
 
 ADD, MUL, MAX, MIN = AluOpType.add, AluOpType.mult, AluOpType.max, AluOpType.min
-EQ, GE, GT, LT = AluOpType.is_equal, AluOpType.is_ge, AluOpType.is_gt, AluOpType.is_lt
+EQ, GE, GT = AluOpType.is_equal, AluOpType.is_ge, AluOpType.is_gt
 AND, SHR = AluOpType.bitwise_and, AluOpType.logical_shift_right
 AF = ActivationFunctionType
 
@@ -114,15 +114,17 @@ def rank_program(g, core, T, topo):
         return tok
 
     others = [s for s in range(4) if s != rank]
+    far = [s for s in others if topo.die(T.cores[s]) != topo.die(core)]
     SHARE = 4
 
     def send(src_of, dst, arr, loc, reads):
         deps("g", reads, [], True)
         tr = []
-        for i, s in enumerate(others):
+        for s in others:
             dstc = T.cores[s]
             a = topo.addr(dstc)
-            eng = topo.engines(core, dstc)[SHARE * i:SHARE * (i + 1)]
+            first = 2 * SHARE * far.index(s) if s in far else 1
+            eng = topo.engines(core, dstc)[first:first + 2 * SHARE:2][:SHARE]
             tr.append(RemoteDMATransfer(dst_ids=[DstId(rid=a[0], pnc=a[1])], dma_engine_mask=sum(1 << k for k in eng),
                                         remote_sem=T.sem[arr], src=src_of(s), dst=dst))
         g.remote_dma_fused(tr, local_sem=T.sem[loc])
@@ -163,60 +165,90 @@ def rank_program(g, core, T, topo):
     rows = slice(32 * rank, 32 * rank + 32)
     dma("y", A3[:, 0:64, :], T.nx[:], [], [all_("srcAn")])
     dma("s", A3[:, 64:128, :], T.w[:], [], [all_("srcAw")])
-    dma("y", T.er[:], T.e[:], [], [all_("er")])
-    dma("s", T.xr[:], T.x[:], [], [all_("xr")])
+    for G in range(8):
+        dma("ys"[G % 2], T.l1r[:, 16 * G:16 * G + 16], T.nx[G, :], [], [("l1r", 16 * G, 16 * G + 16)])
     dma("y", T.landA[rank, 0:64, :], T.nx[own, :], [], [all_("landAn")])
     dma("s", T.landA[rank, 64:128, :], T.w[own, :], [], [all_("landAw")])
+    dma("y", T.er[:], T.e[:], [], [all_("er")])
+    dma("y", T.xr[:], T.x[:], [], [all_("xr")])
 
-    op("g", lambda e: e.iota(T.kq[:], [[0, 10]], 0, 1), [], [all_("kq")])
+    op("g", lambda e: e.iota(T.kq[:], [[0, 8]], 0, 1), [], [all_("kq")])
     op("g", iota(T.rm[:], [[1, 144]]), [], [all_("rm")])
-    op("g", iota(T.r16[:], [[0, 8], [1, 16]]), [], [all_("r16")])
     op("g", iota(T.r64[:], [[0, 2], [1, 64]]), [], [all_("r64")])
-    tok = op("g", iota(T.r8[:], [[0, 2], [1, 8]]), [], [all_("r8")])
+    op("g", iota(T.r8[:], [[0, 2], [1, 8]]), [], [all_("r8")])
     arrA = send(lambda s: A3[s], T.landA[rank], "arrA", "locA", [all_("srcAn"), all_("srcAw")])
-    tokp = op("g", lambda e: e.iota(T.s2r[64:96, :], [[1, 512]], 0, 512), [], [all_("s2i")], [tok])
 
-    op("v", fill(T.r0[:], 0), [], [all_("r0n"), all_("r0w")])
     kf, cf = T.kf, T.cf
-    PF = [(AND, 127), (AND, 15), (AND, 112), (AND, 3), (SHR, 4, AND, 1), (SHR, 4), (AND, 7), (SHR, 3, AND, 1), (SHR, 2, AND, 1), (SHR, 6)]
+    op("v", fill(T.seg[:], 1.0), [], [all_("seg")])
+    op("v", fill(T.eu[:], 0), [], [all_("eu")])
+    op("v", fill(T.seg[:, 0:256:16], 0.0), [], [all_("seg")])
+    PF = [(AND, 127), (AND, 15), (AND, 112), (SHR, 4, AND, 1), (SHR, 4), (AND, 7), (SHR, 3, AND, 1)]
     for i, f in enumerate(PF):
         kc, kq = T.kc[:, i:i + 1], T.kq[:, i:i + 1]
         op("v", ts(kc, kq, f[1], None, f[0]) if len(f) == 2 else ts(kc, kq, f[1], f[3], f[0], f[2]), [all_("kq")], [("kc", i, i + 1)])
-    op("v", cp(kf[:], T.kc[:]), [all_("kc")], [all_("kf")])
+    op("v", cp(kf[:, 0:7], T.kc[:, 0:7]), [all_("kc")], [all_("kf")])
     KF, RM = all_("kf"), all_("rm")
     names = {}
 
-    def k(i):
-        return kf[:, i:i + 1]
-
     def col(n):
-        return cf[:, names[n]:names[n] + 1]
+        return kf[:, n:n + 1] if n in range(8) else cf[:, names[n]:names[n] + 1]
 
-    def ck(n):
-        return ("cf", names[n], names[n] + 1)
+    def ck(*ns):
+        return [KF] + [("cf", names[n], names[n] + 1) for n in ns if n in names]
 
     def cts(n, in0, s1, s2, *ops):
-        def val(a):
-            if isinstance(a, str):
-                return k(int(a[1:])) if a[1:].isdigit() else col(a)
-            return a
-        rd = [KF] + [ck(a) for a in (in0, s1, s2) if isinstance(a, str) and not a[1:].isdigit()]
-        args = (val(in0), val(s1), val(s2))
+        args = [a if a is None or isinstance(a, float) else col(a) for a in (in0, s1, s2)]
+        rd = ck(in0, s1, s2)
         names[n] = len(names)
-        op("v", ts(col(n), args[0], args[1], args[2], *ops), rd, [ck(n)])
+        op("v", ts(col(n), args[0], args[1], args[2], *ops), rd, ck(n)[1:])
 
     def match(out, okey, row, rkey, at, on=None):
-        rd = [rkey, KF] + [ck(a) for a in (at, on) if a in names]
-        a = col(at) if at in names else k(int(at[1:]))
         if on is None:
-            op("v", ts(out, row, a, None, EQ), rd, [okey])
+            op("v", ts(out, row, col(at), None, EQ), [rkey] + ck(at), [okey])
         else:
-            op("v", ts(out, row, a, col(on) if on in names else k(int(on[1:])), EQ, MUL), rd, [okey])
+            op("v", ts(out, row, col(at), col(on), EQ, MUL), [rkey] + ck(at, on), [okey])
 
-    cts("y0", "k4", -1.0, 1.0, MUL, ADD)
-    op("v", fill(T.eu[:], 0), [], [all_("eu")])
-    op("v", ts(T.ed[:, :, 0:16], T.er[:, :, 16:32], col("y0"), None, MUL), [all_("er"), ck("y0")], [("ed", 0, 1)])
-    op("v", ts(T.ed[:, :, 16:32], T.er[:, :, 16:32], k(4), None, MUL), [all_("er"), KF], [("ed", 1, 2)])
+    STEP = ((1, 1.0), (2, 2.0), (4, 3.5))
+    cts("row0", 1, 0.0, None, EQ)
+    cts("ja", 6, -7.5, 1, MUL, ADD)
+    cts("c15", 2, 15.0, None, ADD)
+    cts("lo8", 6, -1.0, 1.0, MUL, ADD)
+    op("v", ts(T.b16[:], T.rm[:, 0:16], 128.0, col("row0"), MUL, MUL), [RM] + ck("row0"), [all_("b16")])
+    for j in range(16):
+        op("s", lambda e, j=j: e.activation(T.r0[:, W * j:W * j + W], T.rm[:, 0:W], AF.Identity, bias=T.b16[:, j:j + 1], scale=col("row0")),
+           [RM, all_("b16")] + ck("row0"), [("r0n", j, j + 1), ("r0w", j, j + 1)])
+    cts("jc", "row0", 100.0, "ja", MUL, ADD)
+    cts("na", 2, 96.0, -128.0, GE, MUL)
+    cts("sa", 4, 8.0, 5, MUL, ADD)
+    cts("pa", 5, 16.0, 4, MUL, ADD)
+    cts("ta", 5, 6, None, ADD)
+    cts("y0", 3, -1.0, 1.0, MUL, ADD)
+    for i, (s, thr) in enumerate(STEP):
+        cts("ra%d" % i, 1, float(s), None, EQ)
+        cts("ma%d" % i, "jc", thr, -1000.0, GT, MUL)
+    match(T.idh[:], all_("idh"), T.rm[:, 0:W], RM, 0)
+    cts("nb", "na", 2, 47.0, ADD, ADD)
+    cts("pb", "pa", 8.0, None, ADD)
+    cts("tb", "lo8", 100.0, "ta", MUL, ADD)
+    for i, (s, thr) in enumerate(STEP):
+        cts("mb%d" % i, "ma%d" % i, 0, float(s), ADD, ADD)
+        match(T.rw[:, 144 * i:144 * i + 144], ("rw", i, i + 1), T.rm[:], RM, "c15", "ra%d" % i)
+    match(T.sw[:], all_("sw"), T.r64[:], all_("r64"), "sa", 6)
+    match(T.rw[:, 432:576], ("rw", 3, 4), T.rm[:], RM, "nb", "lo8")
+    for i in range(3):
+        match(T.mg[:, W * i:W * i + W], ("mg", i, i + 1), T.rm[:, 0:W], RM, "mb%d" % i)
+    for h in range(2):
+        for h2 in range(2):
+            i = 2 * h + h2
+            match(T.pm[:, W * i:W * i + W], ("pm", i, i + 1), T.rm[:, 0:W], RM, ("pa", "pb")[h], ("lo8", 6)[h2])
+    op("v", ts(T.mtab[:], T.r8[:], col("tb"), col("ta"), MIN, EQ), [all_("r8")] + ck("ta", "tb"), [all_("mtab")])
+
+    op("v", cp(T.l1h[:], T.l1r[:]), [all_("l1r")], [all_("l1h")])
+    op("v", cp(T.l1f[:, rows], T.l1r[:, rows]), [all_("l1r")], [all_("l1f")])
+    arrL = send(lambda s: T.l1h[:, 32 * s:32 * s + 32], T.l1f[:, rows], "arrL", "locL", [all_("l1h")])
+
+    op("v", ts(T.ed[:, :, 0:16], T.er[:, :, 16:32], col("y0"), None, MUL), [all_("er")] + ck("y0"), [("ed", 0, 1)])
+    op("v", ts(T.ed[:, :, 16:32], T.er[:, :, 16:32], col(3), None, MUL), [all_("er"), KF], [("ed", 1, 2)])
     op("v", ts(T.xo[:], T.er[:, 0, 0:16], 8, M, GE, MUL), [all_("er")], [all_("xo")])
     op("v", cp(T.eu[:, :, 0:16], T.er[:, :, 0:16]), [all_("er")], [("eu", 0, 1)])
     op("v", lambda e: e.transpose(T.et[:], T.ed[:]), [all_("ed")], [all_("et")])
@@ -225,58 +257,14 @@ def rank_program(g, core, T, topo):
     op("v", cp(T.eu[:, 0, 32:48], T.xs[:]), [all_("xs")], [("eu", 1, 2)])
     op("v", cp(T.eu[:, :, 16:32], T.es[:]), [all_("es")], [("eu", 2, 3)])
     dma("y", T.srcE[:], T.eu[:], [all_("eu")], [all_("srcE")])
-    dma("s", T.landE[rank], T.eu[rows, :, :], [all_("eu")], [all_("landE")])
+
+    R0K = [all_("r0n"), all_("r0w")]
+    dma("y", T.r0[1:128:16, :], T.landA[:, 0:64, :], [all_("landAn")], R0K[:1], [arrA])
+    dma("s", T.r0[8:128:16, :], T.landA[:, 64:128, :], [all_("landAw")], R0K[1:], [arrA])
+    dma("y", T.landE[rank], T.eu[rows, :, :], [all_("eu")], [all_("landE")])
     arrE = send(lambda s: T.srcE[s], T.landE[rank], "arrE", "locE", [all_("srcE")])
-    op("g", iota(T.tab[:, 0:M], [[0, M]]), [], [("tab", 0, M)], [tokp])
-
-    match(T.idh[:], all_("idh"), T.rm[:, 0:W], RM, "k0")
-    cts("la", "k5", 32.0, 1.0, MUL, ADD)
-    cts("lb", "k8", 16.0, "la", MUL, ADD)
-    cts("lc", "k7", 7.0, "lb", MUL, ADD)
-    op("v", ts(T.lb[0:64, :], T.rm[0:64, 0:W], cf[0:64, names["lc"]:names["lc"] + 1], None, EQ), [RM, ck("lc")], [("lb", 0, 1)])
-    op("v", ts(T.lb[64:128, :], T.r16[64:128, :], 0.0, None, EQ), [all_("r16")], [("lb", 1, 2)])
-    for v in range(4):
-        cts("v%d_" % v, "k3", float(v), None, EQ)
-    for v in range(4):
-        op("v", ts(T.lbv[:, W * v:W * v + W], T.lb[:], col("v%d_" % v), None, MUL), [all_("lb"), ck("v%d_" % v)], [("lbv", W * v, W * v + W)])
-    cts("ja", "k7", -7.5, "k1", MUL, ADD)
-    cts("jb", "k1", 0.0, 100.0, EQ, MUL)
-    cts("jc", "ja", "jb", None, ADD)
-    cts("c15", "k2", 15.0, None, ADD)
-    STEP = ((1, 1.0), (2, 2.0), (4, 3.5))
-    for i, (s, thr) in enumerate(STEP):
-        cts("ma%d_" % i, "jc", thr, -1000.0, GT, MUL)
-        cts("ra%d_" % i, "k1", float(s), None, EQ)
-    for i, (s, thr) in enumerate(STEP):
-        cts("mb%d_" % i, "ma%d_" % i, "k0", float(s), ADD, ADD)
-        match(T.rw[:, 144 * i:144 * i + 144], ("rw", i, i + 1), T.rm[:], RM, "c15", "ra%d_" % i)
-    for i in range(3):
-        match(T.mg[:, W * i:W * i + W], ("mg", i, i + 1), T.rm[:, 0:W], RM, "mb%d_" % i)
-    cts("lo8", "k7", -1.0, 1.0, MUL, ADD)
-    cts("na", "k2", 96.0, -128.0, GE, MUL)
-    cts("nb", "na", "k2", 47.0, ADD, ADD)
-    cts("sa", "k5", 8.0, "k6", MUL, ADD)
-    cts("pa", "k6", 16.0, "k5", MUL, ADD)
-    cts("pb", "pa", 8.0, None, ADD)
-    cts("ta", "k6", "k7", None, ADD)
-    cts("tb", "lo8", 100.0, "ta", MUL, ADD)
-    match(T.rw[:, 432:576], ("rw", 3, 4), T.rm[:], RM, "nb", "lo8")
-    match(T.sw[:], all_("sw"), T.r64[:], all_("r64"), "sa", "k7")
-    for h in range(2):
-        for h2 in range(2):
-            i = 2 * h + h2
-            match(T.pm[:, W * i:W * i + W], ("pm", i, i + 1), T.rm[:, 0:W], RM, ("pa", "pb")[h], ("lo8", "k7")[h2])
-    op("v", ts(T.mtab[:], T.r8[:], col("tb"), col("ta"), MIN, EQ), [all_("r8"), ck("ta"), ck("tb")], [all_("mtab")])
-    op("v", fill(T.seg[:], 1.0), [], [all_("seg")])
-    op("v", fill(T.seg[:, 0:256:16], 0.0), [], [all_("seg")])
-
-    LA = [all_("landAn"), all_("landAw")]
-    for G in range(8):
-        q, y = G // 2, G % 2
-        dma("sy"[y], T.l1r[:, 16 * G:16 * G + 16], T.landA[q, 32 * y:32 * y + 32, :], LA[:1], [("l1r", 16 * G, 16 * G + 16)], [arrA])
-    dma("y", T.r0[1:128:16, :], T.landA[:, 0:64, :], LA[:1], [all_("r0n")], [arrA])
-    dma("s", T.r0[8:128:16, :], T.landA[:, 64:128, :], LA[1:], [all_("r0w")], [arrA])
-    dma("y", T.s2r[0:64, :], T.landA[:], LA, [all_("s2m")], [arrA])
+    op("g", lambda e: e.affine_select(T.k0[:], T.r0[:, 512:1024], [[0, 512]], GE, 0.0, 0, 0), R0K, [all_("k0")])
+    op("g", iota(T.tab[:, 0:M], [[0, M]]), [], [("tab", 0, M)])
     for t in range(4):
         for r0, r1, sh in ((0, 4 - t, t), (4 - t, 4, t - 4)):
             if r0 < r1:
@@ -284,17 +272,10 @@ def rank_program(g, core, T, topo):
                     T.landE[r0:r1, t // 2::2, 16 * (t % 2):16 * (t % 2) + 16], [all_("landE")], [("ep", 2 * t + (r0 > 0), 2 * t + (r0 > 0) + 1)], [arrE])
     dma("y", T.ql0[:], T.landE[:, 0::4, 32:48], [all_("landE")], [all_("ql0")], [arrE])
 
-    op("v", cp(T.l1f[:], T.l1r[:]), [all_("l1r")], [all_("l1f")])
-    op("p", mm(T.pb6[:, 0:W], T.l1f[:], T.idh[:]), [all_("l1f"), all_("idh")], [("pb6", 0, 1)])
+    op("p", mm(T.pb6[:, 0:W], T.l1f[:], T.idh[:]), [all_("l1f"), all_("idh")], [("pb6", 0, 1)], [arrL])
     op("v", cp(T.l1[:], T.pb6[:, 0:W]), [("pb6", 0, 1)], [all_("l1")])
-    op("s", act(T.s2f[0:96, :], T.s2r[0:96, :]), [all_("s2m"), all_("s2i")], [all_("s2f")])
-    TB = ["pb0", "pb1", "pb2", "pb3"]
 
-    def first(c):
-        op("p", mm(T[TB[c]][:], T.lbv[0:68, W * c:W * c + W], T.s2f[0:68, :], True, False),
-           [("lbv", W * c, W * c + W), all_("s2f")], [(TB[c], 0, 1)])
-    for c in range(4):
-        first(c)
+    TB, GK = ["pb0", "pb1", "pb2", "pb3"], ["ga", "gb", "gc"]
 
     def gather(q, out, okey, o0, lo, hi, win, wkeys, lst):
         op(q, move(q, out[:, o0 + lo:o0 + hi], win.indirect(T[lst][:, lo // 16:hi // 16])),
@@ -304,15 +285,13 @@ def rank_program(g, core, T, topo):
         b = "pb%d" % (4 + h)
         op(q, move(q, T[lst][:, 64 * h:64 * h + 64], T[b][:, 0:64]), [(b, 0, 1)], [(lst, 64 * h, 64 * h + 64)])
 
-    GK = ["ga", "gb", "gc"]
-
     def level(i, win, wkeys, lst, dst, d0, nxt):
         gk = GK[i]
 
         def piece(q, lo, hi):
-            gather(q, T[gk], gk, 0, lo, hi, win, wkeys, lst)
+            gather(q, T[gk], gk, 0, lo, hi, T[win][:], wkeys, lst)
 
-        def merge(lo, hi, start, j=i):
+        def merge(lo, hi, start=True, j=i):
             c = lo // 512
             op("p", mm(T[TB[c]][:, lo - 512 * c:hi - 512 * c], T.mg[:, W * j:W * j + W], T[GK[j]][:, lo:hi], start, j == i),
                [("mg", j, j + 1), (GK[j], lo, hi)], [(TB[c], 0, 1)])
@@ -323,72 +302,61 @@ def rank_program(g, core, T, topo):
                 op("p", mm(T[b][:, 0:64], T.rw[:, 144 * i + 15 - r:144 * i + 143 - r], T[gk][:, 1024 * h + r:1024 * h + 1024:16], r == 0, r == 15),
                    [("rw", i, i + 1), (gk, 1024 * h, 1024 * h + 1024)], [(b, 0, 1)])
 
-        def out(q, lo, hi, add=False):
+        def out(lo, hi):
             c = lo // 512
-            src = T[TB[c]][:, lo - 512 * c:hi - 512 * c]
-            if add:
-                op("v", tt(T[dst][:, d0 + lo:d0 + hi], T[wkeys[0][0]][:, lo:hi], src, ADD), [(TB[c], 0, 1)] + wkeys, [(dst, d0 + lo, d0 + hi)])
-            else:
-                op(q, move(q, T[dst][:, d0 + lo:d0 + hi], src), [(TB[c], 0, 1)], [(dst, d0 + lo, d0 + hi)])
-        if i == 0:
-            for q, lo in (("v", 0), ("s", 512), ("v", 1024), ("s", 1536)):
-                piece(q, lo, lo + 512)
-            merge(0, 512, False)
-            merge(512, 1024, False)
-            relay(0, 0, 8)
-            merge(1024, 1536, False)
-            merge(1536, M, False)
-            relay(0, 8, 16)
-            out("v", 0, 512)
-            out("s", 512, 1024)
-            out("v", 1024, 1536)
-            out("s", 1536, M)
-            relist(0, nxt)
-            relay(1)
-            return
+            op("v", tt(T[dst][:, d0 + lo:d0 + hi], T[win][:, lo:hi], T[TB[c]][:, lo - 512 * c:hi - 512 * c], ADD),
+               [(TB[c], 0, 1)] + wkeys, [(dst, d0 + lo, d0 + hi)])
+
+        def old():
+            op("p", mm(T.pb1[:], T.idh[:], T.k0[:], True, False), [all_("idh"), all_("k0")], [("pb1", 0, 1)])
+            for j in range(i):
+                merge(512, 1024, False, j)
         piece("v", 0, 256)
         piece("s", 512, 1024)
-        relist(1, lst)
+        if i > 0:
+            relist(1, lst)
         piece("v", 256, 512)
         piece("v", 1024, CUT)
         piece("s", 1536, M)
         piece("s", CUT, 1536)
-        first(1)
-        for j in range(i):
-            merge(512, 1024, False, j)
-        merge(0, 512, True)
-        merge(512, 1024, False)
-        merge(1024, CUT, True)
-        out("v", 0, 512, True)
-        out("v", 1024, CUT, True)
-        relay(0, 0, 6)
-        merge(1536, M, True)
-        relay(0, 6, 16)
-        merge(CUT, 1536, True)
-        out("s", 512, 1024)
-        out("v", 1536, M, True)
-        relist(0, nxt, RQ)
-        out("v", CUT, 1536, True)
+        if i > 0:
+            old()
+        merge(0, 512)
+        if i > 0:
+            merge(512, 1024, False)
+        merge(1024, CUT)
+        out(0, 512)
+        out(1024, CUT)
+        relay(0, 0, R0)
+        merge(1536, M)
+        if i == 0:
+            old()
+            merge(512, 1024, False)
+        else:
+            relay(0, R0, R1)
+        merge(CUT, 1536)
+        relay(0, R0 if i == 0 else R1, 16)
+        op("s", act(T[dst][:, d0 + 512:d0 + 1024], T.pb1[:]), [("pb1", 0, 1)], [(dst, d0 + 512, d0 + 1024)])
+        out(1536, M)
+        relist(0, nxt, "s")
+        out(CUT, 1536)
         relay(1)
 
-    level(0, T.r0[:], [all_("r0n"), all_("r0w")], "l1", "t1", 0, "l2")
-    level(1, T.t1[:], [all_("t1")], "l2", "t2", 0, "l4")
-    level(2, T.t2[:], [all_("t2")], "l4", "tab", M, "l8")
-
-    def elist(t):
-        return T.ep[:, t // 4, 16 * (t % 4):16 * (t % 4) + 16]
+    level(0, "r0", R0K, "l1", "t1", 0, "l2")
+    level(1, "t1", [all_("t1")], "l2", "t2", 0, "l4")
+    level(2, "t2", [all_("t2")], "l4", "tab", M, "l8")
 
     def mask(t):
-        op("s", act(T.em[:, 256 * t:256 * t + 256], T.mtab[:].indirect(elist(t))), [all_("mtab"), all_("ep")], [("em", 256 * t, 256 * t + 256)])
+        lst = T.ep[:, t // 4, 16 * (t % 4):16 * (t % 4) + 16]
+        op("s", act(T.em[:, 256 * t:256 * t + 256], T.mtab[:].indirect(lst)), [all_("mtab"), all_("ep")], [("em", 256 * t, 256 * t + 256)])
     A, AK = T.tab[:, M:2 * M], [("tab", M, 2 * M)]
-    NV = 1184
     gather("v", T.tab, "tab", 2 * M, 0, 256, A, AK, "l8")
     gather("s", T.tab, "tab", 2 * M, 512, 1024, A, AK, "l8")
     relist(1, "l8")
     gather("v", T.tab, "tab", 2 * M, 256, 512, A, AK, "l8")
     op("v", ts(T.off[:], T.ep[:], 8, M, GE, MUL), [all_("ep")], [all_("off")])
-    gather("v", T.tab, "tab", 2 * M, 1024, 512 + NV, A, AK, "l8")
-    gather("s", T.tab, "tab", 2 * M, 512 + NV, M, A, AK, "l8")
+    gather("v", T.tab, "tab", 2 * M, 1024, C2, A, AK, "l8")
+    gather("s", T.tab, "tab", 2 * M, C2, M, A, AK, "l8")
     mask(0)
 
     PL, PW = ["pb4", "pb5"], ["pb6", "pb7"]
@@ -411,47 +379,60 @@ def rank_program(g, core, T, topo):
             op("p", mm(T[b][:, 0:16], T.rw[:, 447 - a:575 - a], T[x][:, 16 * a:16 * a + 16], t == 7 and a == 0, a == 15),
                [("rw", 3, 4), (x, W * h, W * h + W)], [(b, 0, 1)])
 
-    def weights(t):
-        x, z, b, c = "x%d" % (t % 2), "z%d" % (t % 2), PW[t % 2], 16 * (t % 4)
-        sel = T.sw[:, c:c + 64]
-        for h in range(2):
-            o = W * h
-            op("p", mm(T[b][:, o + 1:o + W:2], T[z][:, o:o + W], sel), [all_(z), all_("sw")], [(b, 0, 1)])
-        for h in range(2):
-            o = W * h
-            op("p", mm(T[b][:, o:o + W:2], T[x][:, o:o + W], sel, True, t == 0), [(x, o, o + W), all_("sw")], [(b, 0, 1)])
-            if t > 0:
-                for h0 in range(2):
-                    i = 2 * h0 + h
-                    op("p", mm(T[b][:, o + 14:o + W:16], T.pm[:, W * i:W * i + W], T.pk[:, W * h0 + 15:W * h0 + W:16], False, h0 == 1),
-                       [("pm", i, i + 1), all_("pk")], [(b, 0, 1)])
+    def wz(t, h):
+        z, b, c, o = "z%d" % (t % 2), PW[t % 2], 16 * (t % 4), W * h
+        op("p", mm(T[b][:, o + 1:o + W:2], T[z][:, o:o + W], T.sw[:, c:c + 64]), [all_(z), all_("sw")], [(b, 0, 1)])
+
+    def wx(t, h):
+        x, b, c, o = "x%d" % (t % 2), PW[t % 2], 16 * (t % 4), W * h
+        carry = 0 < t < 7
+        op("p", mm(T[b][:, o:o + W:2], T[x][:, o:o + W], T.sw[:, c:c + 64], True, not carry), [(x, o, o + W), all_("sw")], [(b, 0, 1)])
+        if carry:
+            for h0 in range(2):
+                i = 2 * h0 + h
+                op("p", mm(T[b][:, o + 14:o + W:16], T.pm[:, W * i:W * i + W], T.pk[:, W * h0 + 15:W * h0 + W:16], False, h0 == 1),
+                   [("pm", i, i + 1), all_("pk")], [(b, 0, 1)])
 
     def scan(t):
-        b = PW[t % 2]
-        op("v", lambda e: e.tensor_tensor_scan(T.pk[:], T.seg[:], T[b][:, 0:256], 0.0, MUL, MAX), [all_("seg"), (b, 0, 1)], [all_("pk")])
+        b, pk = PW[t % 2], "pk7" if t == 7 else "pk"
+        op("v", lambda e: e.tensor_tensor_scan(T[pk][:], T.seg[:], T[b][:, 0:256], 0.0, MUL, MAX), [all_("seg"), (b, 0, 1)], [all_(pk)])
 
-    for t in range(8):
+    for t in range(7):
         look(t, 0)
         early(t)
         places(t, 0)
         look(t, 1)
         places(t, 1)
-        if t < 7:
-            mask(t + 1)
+        mask(t + 1)
         if t > 0:
             scan(t - 1)
-        weights(t)
-        b = PL[t % 2]
-        if t < 7:
-            q = "ql%d" % ((t + 1) % 2)
-            op("v", cp(T[q][:], T[b][:, 0:16]), [(b, 0, 1)], [all_(q)])
-        else:
-            op("s", act(T.outb[:, 0:16], T[b][:, 0:16]), [(b, 0, 1)], [("outb", 0, 16)])
+        wz(t, 0)
+        wz(t, 1)
+        wx(t, 0)
+        wx(t, 1)
+        b, q = PL[t % 2], "ql%d" % ((t + 1) % 2)
+        op("v", cp(T[q][:], T[b][:, 0:16]), [(b, 0, 1)], [all_(q)])
+    look(7, 0)
+    early(7)
+    look(7, 1)
+    wx(7, 0)
+    places(7, 0)
+    wz(7, 0)
+    wz(7, 1)
+    wx(7, 1)
+    scan(6)
     scan(7)
+    for r in range(16):
+        for h in range(2):
+            o = W * (2 * h + r // 8) + 16 * (r % 8)
+            op("p", mm(T.pb2[0:16, r:W:16], T.pm[:, o:o + 16], T.pk[:, W * h + 15:W * h + W:16], h == 0, h == 1), [all_("pm"), all_("pk")], [("pb2", 0, 1)])
+    op("s", act(T.y6[0:16, :], T.pb2[0:16, 0:W]), [("pb2", 0, 1)], [all_("y6")])
     for h in range(2):
         for r in range(8):
-            op("p", mm(T.pb0[0:16, 8 * h + r:W:16], T.idh[:, 16 * r:16 * r + 16], T.pk[:, W * h + 15:W * h + W:16]), [all_("idh"), all_("pk")], [("pb0", 0, 1)])
-    op("v", cp(T.yw[0:16, :], T.pb0[0:16, 0:W]), [("pb0", 0, 1)], [all_("yw")])
+            op("p", mm(T.pb0[0:16, 8 * h + r:W:16], T.idh[:, 16 * r:16 * r + 16], T.pk7[:, W * h + 15:W * h + W:16]), [all_("idh"), all_("pk7")], [("pb0", 0, 1)])
+    places(7, 1)
+    op("v", tt(T.yw[0:16, :], T.y6[0:16, :], T.pb0[0:16, 0:W], MAX), [("pb0", 0, 1), all_("y6")], [all_("yw")])
+    op("s", act(T.outb[:, 0:16], T[PL[1]][:, 0:16]), [(PL[1], 0, 1)], [("outb", 0, 16)])
     op("p", mm(T.pb1[:, 0:16], T.yw[0:16, :], T.idh[0:16, 0:16]), [all_("yw"), all_("idh")], [("pb1", 0, 1)])
     op("v", cp(T.outb[:, 16:32], T.pb1[:, 0:16]), [("pb1", 0, 1)], [("outb", 16, 32)])
 

@@ -3,15 +3,21 @@ from concourse.mybir import AluOpType, ActivationFunctionType
 
 ND = 40
 M = 2048
-CUT, C2, R0, R1 = 1280, 1696, 4, 10
+CUTS = (1312, 1312, 1312, 1504)
+TURNS = ((0, 0, 6), (2, 6, 12), (2, 6, 12))
+HEAD = 320
+MASK0 = (0, 6, 12, 16)
+LK = (0, 96, 192, 256)
+SA = 4
 SCRATCH = {
     "srcA": ("dram", [4, 128, 64], "int32"), "srcE": ("dram", [4, 128, 48], "uint16"),
-    "landA": ("dram", [4, 128, 64], "int32"), "landE": ("dram", [4, 128, 48], "uint16"), "landO": ("dram", [4, 128, 32], "float32"),
+    "landA": ("dram", [4, 128, 64], "int32"), "landE": ("dram", [4, 128, 48], "uint16"),
+    "landL": ("dram", [4, 128, 16], "float32"), "landP": ("dram", [4, 128, 16], "float32"),
     "er": ("sbuf", [128, 4, 32], "int32"), "xr": ("sbuf", [128, 16], "int32"), "ed": ("sbuf", [128, 4, 32], "bfloat16"),
     "et": ("sbuf", [128, 4, 32], "bfloat16"), "es": ("sbuf", [128, 4, 16], "bfloat16"), "eu": ("sbuf", [128, 4, 48], "uint16"),
     "xo": ("sbuf", [128, 16], "float32"), "xs": ("sbuf", [128, 16], "float32"),
     "r0": ("sbuf", [128, M], "int32"), "k0": ("sbuf", [128, 512], "float16"),
-    "l1r": ("sbuf", [128, 128], "int32"), "l1h": ("sbuf", [128, 128], "float16"), "l1f": ("sbuf", [128, 128], "float16"),
+    "l1r": ("sbuf", [128, 4, 32], "int32"), "l1h": ("sbuf", [128, 4, 64], "float16"), "l1f": ("sbuf", [128, 256], "float16"),
     "t1": ("sbuf", [128, M], "float32"), "t2": ("sbuf", [128, M], "float32"), "tab": ("sbuf", [128, 3 * M], "float32"),
     "ga": ("sbuf", [128, M], "float16"), "gb": ("sbuf", [128, M], "float16"), "gc": ("sbuf", [128, M], "float16"),
     "l1": ("sbuf", [128, 128], "uint16"), "l2": ("sbuf", [128, 128], "uint16"), "l4": ("sbuf", [128, 128], "uint16"), "l8": ("sbuf", [128, 128], "uint16"),
@@ -20,16 +26,17 @@ SCRATCH = {
     "x0": ("sbuf", [128, 256], "float16"), "x1": ("sbuf", [128, 256], "float16"),
     "z0": ("sbuf", [128, 256], "float16"), "z1": ("sbuf", [128, 256], "float16"),
     "pk": ("sbuf", [128, 256], "float16"), "pk7": ("sbuf", [128, 256], "float16"),
-    "yw": ("sbuf", [128, 128], "float16"), "y6": ("sbuf", [128, 128], "float16"), "outb": ("sbuf", [128, 32], "float32"),
-    "kq": ("sbuf", [128, 8], "int32"), "kc": ("sbuf", [128, 8], "int32"), "kf": ("sbuf", [128, 8], "float32"), "cf": ("sbuf", [128, 40], "float32"),
+    "yw": ("sbuf", [128, 128], "float16"), "y6": ("sbuf", [128, 128], "float16"),
+    "outl": ("sbuf", [128, 16], "float32"), "outp": ("sbuf", [128, 16], "float32"),
+    "kq": ("sbuf", [128, 10], "int32"), "kc": ("sbuf", [128, 10], "int32"), "kf": ("sbuf", [128, 10], "float32"), "cf": ("sbuf", [128, 40], "float32"),
     "rm": ("sbuf", [128, 144], "bfloat16"), "r64": ("sbuf", [128, 128], "bfloat16"), "r8": ("sbuf", [128, 16], "bfloat16"),
-    "b16": ("sbuf", [128, 16], "float32"), "idh": ("sbuf", [128, 128], "float16"),
+    "b16": ("sbuf", [128, 16], "float32"), "d64": ("sbuf", [128, 64], "float16"), "idh": ("sbuf", [128, 128], "float16"),
     "mg": ("sbuf", [128, 384], "float16"), "rw": ("sbuf", [128, 576], "float16"), "sw": ("sbuf", [128, 128], "float16"),
     "pm": ("sbuf", [128, 512], "float16"), "seg": ("sbuf", [128, 256], "bfloat16"), "mtab": ("sbuf", [128, 16], "bfloat16"),
 }
 for _i in range(8):
     SCRATCH["pb%d" % _i] = ("psum", [128, 512], "float32")
-SEMAPHORES = ["vv", "ss", "pp", "gq", "arrA", "arrL", "arrE", "arrO", "locA", "locL", "locE", "locO"] + ["d%d" % _i for _i in range(ND)]
+SEMAPHORES = ["vv", "ss", "pp", "gq", "arrA", "arrL", "arrE", "arrO", "arrP", "locA", "locL", "locE", "locO", "locP"] + ["d%d" % _i for _i in range(ND)]
 
 ADD, MUL, MAX, MIN = AluOpType.add, AluOpType.mult, AluOpType.max, AluOpType.min
 EQ, GE, GT = AluOpType.is_equal, AluOpType.is_ge, AluOpType.is_gt
@@ -117,20 +124,27 @@ def rank_program(g, core, T, topo):
     far = [s for s in others if topo.die(T.cores[s]) != topo.die(core)]
     SHARE = 4
 
-    def send(src_of, dst, arr, loc, reads):
+    def send(src_of, dst, arr, loc, reads, near=1, n=SHARE):
         deps("g", reads, [], True)
         tr = []
         for s in others:
-            dstc = T.cores[s]
-            a = topo.addr(dstc)
-            first = 2 * SHARE * far.index(s) if s in far else 1
-            eng = topo.engines(core, dstc)[first:first + 2 * SHARE:2][:SHARE]
+            a = topo.addr(T.cores[s])
+            first = 2 * SHARE * far.index(s) if s in far else near
+            eng = topo.engines(core, T.cores[s])[first::2][:n]
             tr.append(RemoteDMATransfer(dst_ids=[DstId(rid=a[0], pnc=a[1])], dma_engine_mask=sum(1 << k for k in eng),
                                         remote_sem=T.sem[arr], src=src_of(s), dst=dst))
         g.remote_dma_fused(tr, local_sem=T.sem[loc])
-        total[loc] = 3 * SHARE
-        total[arr] = 3 * SHARE
-        return (arr, 3 * SHARE, {})
+        total[loc] = total[arr] = 3 * n
+        return (arr, 3 * n, {})
+
+    def send_all(src, dst, arr, loc, reads):
+        deps("g", reads, [], True)
+        ads = [topo.addr(T.cores[s]) for s in others]
+        n = len(topo.engines(core, T.cores[others[0]]))
+        g.remote_dma_fused([RemoteDMATransfer(dst_ids=[DstId(rid=a[0], pnc=a[1]) for a in ads], dma_engine_mask=topo.mask(core, T.cores[others[0]]),
+                                              remote_sem=T.sem[arr], srcs=[src], dsts=[dst] * 3)], local_sem=T.sem[loc])
+        total[loc], total[arr] = n, 3 * n
+        return (arr, 3 * n, {})
 
     def ts(out, in0, s1, s2, *ops):
         return lambda e: e.tensor_scalar(out, in0, s1, s2, *ops)
@@ -165,33 +179,33 @@ def rank_program(g, core, T, topo):
     rows = slice(32 * rank, 32 * rank + 32)
     dma("y", A3[:, 0:64, :], T.nx[:], [], [all_("srcAn")])
     dma("s", A3[:, 64:128, :], T.w[:], [], [all_("srcAw")])
-    for G in range(8):
-        dma("ys"[G % 2], T.l1r[:, 16 * G:16 * G + 16], T.nx[G, :], [], [("l1r", 16 * G, 16 * G + 16)])
+    dma("y", T.er[:], T.e[:], [], [all_("er")])
+    dma("s", T.xr[:], T.x[:], [], [all_("xr")])
+    for s in range(4):
+        dma("ys"[s % 2], T.l1r[:, s, :], T.nx[2 * s:2 * s + 2, :], [], [("l1r", s, s + 1)])
     dma("y", T.landA[rank, 0:64, :], T.nx[own, :], [], [all_("landAn")])
     dma("s", T.landA[rank, 64:128, :], T.w[own, :], [], [all_("landAw")])
-    dma("y", T.er[:], T.e[:], [], [all_("er")])
-    dma("y", T.xr[:], T.x[:], [], [all_("xr")])
 
-    op("g", lambda e: e.iota(T.kq[:], [[0, 8]], 0, 1), [], [all_("kq")])
+    op("g", lambda e: e.iota(T.kq[:], [[0, 10]], 0, 1), [], [all_("kq")])
     op("g", iota(T.rm[:], [[1, 144]]), [], [all_("rm")])
     op("g", iota(T.r64[:], [[0, 2], [1, 64]]), [], [all_("r64")])
     op("g", iota(T.r8[:], [[0, 2], [1, 8]]), [], [all_("r8")])
-    arrA = send(lambda s: A3[s], T.landA[rank], "arrA", "locA", [all_("srcAn"), all_("srcAw")])
+    arrA = send(lambda s: A3[s], T.landA[rank], "arrA", "locA", [all_("srcAn"), all_("srcAw")], 1, SA)
 
     kf, cf = T.kf, T.cf
     op("v", fill(T.seg[:], 1.0), [], [all_("seg")])
     op("v", fill(T.eu[:], 0), [], [all_("eu")])
     op("v", fill(T.seg[:, 0:256:16], 0.0), [], [all_("seg")])
-    PF = [(AND, 127), (AND, 15), (AND, 112), (SHR, 4, AND, 1), (SHR, 4), (AND, 7), (SHR, 3, AND, 1)]
+    PF = [(AND, 127), (AND, 15), (AND, 112), (SHR, 4, AND, 1), (SHR, 4), (AND, 7), (SHR, 3, AND, 1), (AND, 63), (SHR, 6)]
     for i, f in enumerate(PF):
         kc, kq = T.kc[:, i:i + 1], T.kq[:, i:i + 1]
         op("v", ts(kc, kq, f[1], None, f[0]) if len(f) == 2 else ts(kc, kq, f[1], f[3], f[0], f[2]), [all_("kq")], [("kc", i, i + 1)])
-    op("v", cp(kf[:, 0:7], T.kc[:, 0:7]), [all_("kc")], [all_("kf")])
+    op("v", cp(kf[:, 0:9], T.kc[:, 0:9]), [all_("kc")], [all_("kf")])
     KF, RM = all_("kf"), all_("rm")
     names = {}
 
     def col(n):
-        return kf[:, n:n + 1] if n in range(8) else cf[:, names[n]:names[n] + 1]
+        return kf[:, n:n + 1] if n in range(10) else cf[:, names[n]:names[n] + 1]
 
     def ck(*ns):
         return [KF] + [("cf", names[n], names[n] + 1) for n in ns if n in names]
@@ -223,13 +237,37 @@ def rank_program(g, core, T, topo):
     cts("pa", 5, 16.0, 4, MUL, ADD)
     cts("ta", 5, 6, None, ADD)
     cts("y0", 3, -1.0, 1.0, MUL, ADD)
+    cts("h0", 8, -1.0, 1.0, MUL, ADD)
+    match(T.d64[:], all_("d64"), T.r64[:, 0:64], all_("r64"), 7)
     for i, (s, thr) in enumerate(STEP):
         cts("ra%d" % i, 1, float(s), None, EQ)
         cts("ma%d" % i, "jc", thr, -1000.0, GT, MUL)
     match(T.idh[:], all_("idh"), T.rm[:, 0:W], RM, 0)
+
+    op("v", ts(T.ed[:, :, 0:16], T.er[:, :, 16:32], col("y0"), None, MUL), [all_("er")] + ck("y0"), [("ed", 0, 1)])
+    op("v", ts(T.ed[:, :, 16:32], T.er[:, :, 16:32], col(3), None, MUL), [all_("er"), KF], [("ed", 1, 2)])
+    op("v", ts(T.xo[:], T.er[:, 0, 0:16], 8, M, GE, MUL), [all_("er")], [all_("xo")])
+    op("v", cp(T.eu[:, :, 0:16], T.er[:, :, 0:16]), [all_("er")], [("eu", 0, 1)])
+    op("v", lambda e: e.transpose(T.et[:], T.ed[:]), [all_("ed")], [all_("et")])
+    op("v", tt(T.xs[:], T.xo[:], T.xr[:], ADD), [all_("xo"), all_("xr")], [all_("xs")])
+    op("v", tt(T.es[:], T.et[:, :, 0:16], T.et[:, :, 16:32], ADD), [all_("et")], [all_("es")])
+    op("v", cp(T.eu[:, 0, 32:48], T.xs[:]), [all_("xs")], [("eu", 1, 2)])
+    op("v", cp(T.eu[:, :, 16:32], T.es[:]), [all_("es")], [("eu", 2, 3)])
+    dma("y", T.srcE[:], T.eu[:], [all_("eu")], [all_("srcE")])
+    dma("y", T.landE[rank], T.eu[rows, :, :], [all_("eu")], [all_("landE")])
+
+    for c in range(2):
+        for y in range(2):
+            o = 32 * y + c
+            op("v", ts(T.l1h[:, :, o:32 * y + 32:2], T.l1r[:, :, 16 * c:16 * c + 16], col(("h0", 8)[y]), None, MUL), [all_("l1r")] + ck("h0"), [("l1h", o, o + 1)])
+    mine = T.l1f[:, 64 * rank:64 * rank + 64]
+    arrL = send(lambda s: T.l1h[:, s, :], mine, "arrL", "locL", [all_("l1h")])
+    arrE = send(lambda s: T.srcE[s], T.landE[rank], "arrE", "locE", [all_("srcE")], 2 * SHARE + 1)
+
     cts("nb", "na", 2, 47.0, ADD, ADD)
     cts("pb", "pa", 8.0, None, ADD)
     cts("tb", "lo8", 100.0, "ta", MUL, ADD)
+    op("v", cp(mine, T.l1h[:, rank, :]), [all_("l1h")], [all_("l1f")])
     for i, (s, thr) in enumerate(STEP):
         cts("mb%d" % i, "ma%d" % i, 0, float(s), ADD, ADD)
         match(T.rw[:, 144 * i:144 * i + 144], ("rw", i, i + 1), T.rm[:], RM, "c15", "ra%d" % i)
@@ -243,26 +281,9 @@ def rank_program(g, core, T, topo):
             match(T.pm[:, W * i:W * i + W], ("pm", i, i + 1), T.rm[:, 0:W], RM, ("pa", "pb")[h], ("lo8", 6)[h2])
     op("v", ts(T.mtab[:], T.r8[:], col("tb"), col("ta"), MIN, EQ), [all_("r8")] + ck("ta", "tb"), [all_("mtab")])
 
-    op("v", cp(T.l1h[:], T.l1r[:]), [all_("l1r")], [all_("l1h")])
-    op("v", cp(T.l1f[:, rows], T.l1r[:, rows]), [all_("l1r")], [all_("l1f")])
-    arrL = send(lambda s: T.l1h[:, 32 * s:32 * s + 32], T.l1f[:, rows], "arrL", "locL", [all_("l1h")])
-
-    op("v", ts(T.ed[:, :, 0:16], T.er[:, :, 16:32], col("y0"), None, MUL), [all_("er")] + ck("y0"), [("ed", 0, 1)])
-    op("v", ts(T.ed[:, :, 16:32], T.er[:, :, 16:32], col(3), None, MUL), [all_("er"), KF], [("ed", 1, 2)])
-    op("v", ts(T.xo[:], T.er[:, 0, 0:16], 8, M, GE, MUL), [all_("er")], [all_("xo")])
-    op("v", cp(T.eu[:, :, 0:16], T.er[:, :, 0:16]), [all_("er")], [("eu", 0, 1)])
-    op("v", lambda e: e.transpose(T.et[:], T.ed[:]), [all_("ed")], [all_("et")])
-    op("v", tt(T.xs[:], T.xo[:], T.xr[:], ADD), [all_("xo"), all_("xr")], [all_("xs")])
-    op("v", tt(T.es[:], T.et[:, :, 0:16], T.et[:, :, 16:32], ADD), [all_("et")], [all_("es")])
-    op("v", cp(T.eu[:, 0, 32:48], T.xs[:]), [all_("xs")], [("eu", 1, 2)])
-    op("v", cp(T.eu[:, :, 16:32], T.es[:]), [all_("es")], [("eu", 2, 3)])
-    dma("y", T.srcE[:], T.eu[:], [all_("eu")], [all_("srcE")])
-
     R0K = [all_("r0n"), all_("r0w")]
     dma("y", T.r0[1:128:16, :], T.landA[:, 0:64, :], [all_("landAn")], R0K[:1], [arrA])
     dma("s", T.r0[8:128:16, :], T.landA[:, 64:128, :], [all_("landAw")], R0K[1:], [arrA])
-    dma("y", T.landE[rank], T.eu[rows, :, :], [all_("eu")], [all_("landE")])
-    arrE = send(lambda s: T.srcE[s], T.landE[rank], "arrE", "locE", [all_("srcE")])
     op("g", lambda e: e.affine_select(T.k0[:], T.r0[:, 512:1024], [[0, 512]], GE, 0.0, 0, 0), R0K, [all_("k0")])
     op("g", iota(T.tab[:, 0:M], [[0, M]]), [], [("tab", 0, M)])
     for t in range(4):
@@ -272,7 +293,8 @@ def rank_program(g, core, T, topo):
                     T.landE[r0:r1, t // 2::2, 16 * (t % 2):16 * (t % 2) + 16], [all_("landE")], [("ep", 2 * t + (r0 > 0), 2 * t + (r0 > 0) + 1)], [arrE])
     dma("y", T.ql0[:], T.landE[:, 0::4, 32:48], [all_("landE")], [all_("ql0")], [arrE])
 
-    op("p", mm(T.pb6[:, 0:W], T.l1f[:], T.idh[:]), [all_("l1f"), all_("idh")], [("pb6", 0, 1)], [arrL])
+    for c in range(2):
+        op("p", mm(T.pb6[:, c:W:2], T.l1f[:, c:256:2], T.d64[:]), [all_("l1f"), all_("d64")], [("pb6", 0, 1)], [arrL])
     op("v", cp(T.l1[:], T.pb6[:, 0:W]), [("pb6", 0, 1)], [all_("l1")])
 
     TB, GK = ["pb0", "pb1", "pb2", "pb3"], ["ga", "gb", "gc"]
@@ -285,15 +307,20 @@ def rank_program(g, core, T, topo):
         b = "pb%d" % (4 + h)
         op(q, move(q, T[lst][:, 64 * h:64 * h + 64], T[b][:, 0:64]), [(b, 0, 1)], [(lst, 64 * h, 64 * h + 64)])
 
+    def mask(t, lo=0, hi=16):
+        c, o = t % 4, 256 * t
+        op("s", act(T.em[:, o + 16 * lo:o + 16 * hi], T.mtab[:].indirect(T.ep[:, t // 4, 16 * c + lo:16 * c + hi])),
+           [all_("mtab"), ("ep", 2 * c, 2 * c + 2)], [("em", o + 16 * lo, o + 16 * hi)])
+
     def level(i, win, wkeys, lst, dst, d0, nxt):
-        gk = GK[i]
+        gk, CUT, (R0, R1, R2) = GK[i], CUTS[i], TURNS[i]
 
         def piece(q, lo, hi):
             gather(q, T[gk], gk, 0, lo, hi, T[win][:], wkeys, lst)
 
-        def merge(lo, hi, start=True, j=i):
+        def merge(lo, hi, start=True, stop=True, j=i):
             c = lo // 512
-            op("p", mm(T[TB[c]][:, lo - 512 * c:hi - 512 * c], T.mg[:, W * j:W * j + W], T[GK[j]][:, lo:hi], start, j == i),
+            op("p", mm(T[TB[c]][:, lo - 512 * c:hi - 512 * c], T.mg[:, W * j:W * j + W], T[GK[j]][:, lo:hi], start, stop),
                [("mg", j, j + 1), (GK[j], lo, hi)], [(TB[c], 0, 1)])
 
         def relay(h, r0=0, r1=16):
@@ -308,63 +335,64 @@ def rank_program(g, core, T, topo):
                [(TB[c], 0, 1)] + wkeys, [(dst, d0 + lo, d0 + hi)])
 
         def old():
-            op("p", mm(T.pb1[:], T.idh[:], T.k0[:], True, False), [all_("idh"), all_("k0")], [("pb1", 0, 1)])
+            op("p", mm(T.pb1[:], T.idh[:], T.k0[:], i > 0, i == 0), [all_("idh"), all_("k0")], [("pb1", 0, 1)])
             for j in range(i):
-                merge(512, 1024, False, j)
-        piece("v", 0, 256)
+                merge(512, 1024, False, False, j)
+        head = HEAD if i else 512
+        piece("v", 0, head)
         piece("s", 512, 1024)
-        if i > 0:
+        if i:
             relist(1, lst)
-        piece("v", 256, 512)
+            piece("v", head, 512)
         piece("v", 1024, CUT)
         piece("s", 1536, M)
         piece("s", CUT, 1536)
-        if i > 0:
+        if i:
             old()
-        merge(0, 512)
-        if i > 0:
-            merge(512, 1024, False)
+        merge(0, head)
+        if i:
+            merge(head, 512)
+        merge(512, 1024, i == 0, i > 0)
+        relay(0, 0, R0)
         merge(1024, CUT)
+        if not i:
+            old()
         out(0, 512)
         out(1024, CUT)
-        relay(0, 0, R0)
+        if i == 2:
+            op("v", ts(T.off[:], T.ep[:], 8, M, GE, MUL), [all_("ep")], [all_("off")])
+        relay(0, R0, R1)
         merge(1536, M)
-        if i == 0:
-            old()
-            merge(512, 1024, False)
-        else:
-            relay(0, R0, R1)
+        relay(0, R1, R2)
         merge(CUT, 1536)
-        relay(0, R0 if i == 0 else R1, 16)
+        relay(0, R2, 16)
         op("s", act(T[dst][:, d0 + 512:d0 + 1024], T.pb1[:]), [("pb1", 0, 1)], [(dst, d0 + 512, d0 + 1024)])
         out(1536, M)
+        if not i:
+            mask(0, MASK0[i], MASK0[i + 1])
         relist(0, nxt, "s")
+        if i:
+            mask(0, MASK0[i], MASK0[i + 1])
         out(CUT, 1536)
         relay(1)
 
     level(0, "r0", R0K, "l1", "t1", 0, "l2")
     level(1, "t1", [all_("t1")], "l2", "t2", 0, "l4")
     level(2, "t2", [all_("t2")], "l4", "tab", M, "l8")
-
-    def mask(t):
-        lst = T.ep[:, t // 4, 16 * (t % 4):16 * (t % 4) + 16]
-        op("s", act(T.em[:, 256 * t:256 * t + 256], T.mtab[:].indirect(lst)), [all_("mtab"), all_("ep")], [("em", 256 * t, 256 * t + 256)])
     A, AK = T.tab[:, M:2 * M], [("tab", M, 2 * M)]
-    gather("v", T.tab, "tab", 2 * M, 0, 256, A, AK, "l8")
+    gather("v", T.tab, "tab", 2 * M, 0, HEAD, A, AK, "l8")
     gather("s", T.tab, "tab", 2 * M, 512, 1024, A, AK, "l8")
     relist(1, "l8")
-    gather("v", T.tab, "tab", 2 * M, 256, 512, A, AK, "l8")
-    op("v", ts(T.off[:], T.ep[:], 8, M, GE, MUL), [all_("ep")], [all_("off")])
-    gather("v", T.tab, "tab", 2 * M, 1024, C2, A, AK, "l8")
-    gather("s", T.tab, "tab", 2 * M, C2, M, A, AK, "l8")
-    mask(0)
+    gather("v", T.tab, "tab", 2 * M, HEAD, 512, A, AK, "l8")
+    gather("v", T.tab, "tab", 2 * M, 1024, CUTS[3], A, AK, "l8")
+    gather("s", T.tab, "tab", 2 * M, CUTS[3], M, A, AK, "l8")
 
     PL, PW = ["pb4", "pb5"], ["pb6", "pb7"]
 
     def look(t, h):
-        q, x, lo = "ql%d" % (t % 2), "x%d" % (t % 2), 256 * t + W * h
-        op("v", tt(T[x][:, W * h:W * h + W], T.tab[:, M:3 * M].indirect(T[q][:, 8 * h:8 * h + 8]), T.em[:, lo:lo + W], MUL),
-           [("tab", M, 3 * M), all_(q), ("em", lo, lo + W)], [(x, W * h, W * h + W)])
+        q, x, lo, hi = "ql%d" % (t % 2), "x%d" % (t % 2), LK[h], LK[h + 1]
+        op("v", tt(T[x][:, lo:hi], T.tab[:, M:3 * M].indirect(T[q][:, lo // 16:hi // 16]), T.em[:, 256 * t + lo:256 * t + hi], MUL),
+           [("tab", M, 3 * M), all_(q), ("em", 256 * t + lo, 256 * t + hi)], [(x, lo, hi)])
 
     def early(t):
         q, z = "ql%d" % (t % 2), "z%d" % (t % 2)
@@ -375,9 +403,9 @@ def rank_program(g, core, T, topo):
         if h == 0 and t < 7:
             n = t + 1
             op("p", mm(T[b][:, 0:16], T.idh[:], T.off[:, n // 4, 16 * (n % 4):16 * (n % 4) + 16], True, False), [all_("idh"), all_("off")], [(b, 0, 1)])
-        for a in range(8 * h, 8 * h + 8):
+        for a in range(LK[h] // 16, LK[h + 1] // 16):
             op("p", mm(T[b][:, 0:16], T.rw[:, 447 - a:575 - a], T[x][:, 16 * a:16 * a + 16], t == 7 and a == 0, a == 15),
-               [("rw", 3, 4), (x, W * h, W * h + W)], [(b, 0, 1)])
+               [("rw", 3, 4), (x, LK[h], LK[h + 1])], [(b, 0, 1)])
 
     def wz(t, h):
         z, b, c, o = "z%d" % (t % 2), PW[t % 2], 16 * (t % 4), W * h
@@ -398,11 +426,10 @@ def rank_program(g, core, T, topo):
         op("v", lambda e: e.tensor_tensor_scan(T[pk][:], T.seg[:], T[b][:, 0:256], 0.0, MUL, MAX), [all_("seg"), (b, 0, 1)], [all_(pk)])
 
     for t in range(7):
-        look(t, 0)
         early(t)
-        places(t, 0)
-        look(t, 1)
-        places(t, 1)
+        for h in range(3):
+            look(t, h)
+            places(t, h)
         mask(t + 1)
         if t > 0:
             scan(t - 1)
@@ -412,16 +439,19 @@ def rank_program(g, core, T, topo):
         wx(t, 1)
         b, q = PL[t % 2], "ql%d" % ((t + 1) % 2)
         op("v", cp(T[q][:], T[b][:, 0:16]), [(b, 0, 1)], [all_(q)])
-    look(7, 0)
     early(7)
-    look(7, 1)
-    wx(7, 0)
+    for h in range(3):
+        look(7, h)
     places(7, 0)
+    places(7, 1)
     wz(7, 0)
     wz(7, 1)
+    wx(7, 0)
     wx(7, 1)
+    places(7, 2)
     scan(6)
     scan(7)
+    op("s", act(T.outl[:], T[PL[1]][:, 0:16]), [(PL[1], 0, 1)], [all_("outl")])
     for r in range(16):
         for h in range(2):
             o = W * (2 * h + r // 8) + 16 * (r % 8)
@@ -430,16 +460,16 @@ def rank_program(g, core, T, topo):
     for h in range(2):
         for r in range(8):
             op("p", mm(T.pb0[0:16, 8 * h + r:W:16], T.idh[:, 16 * r:16 * r + 16], T.pk7[:, W * h + 15:W * h + W:16]), [all_("idh"), all_("pk7")], [("pb0", 0, 1)])
-    places(7, 1)
     op("v", tt(T.yw[0:16, :], T.y6[0:16, :], T.pb0[0:16, 0:W], MAX), [("pb0", 0, 1), all_("y6")], [all_("yw")])
-    op("s", act(T.outb[:, 0:16], T[PL[1]][:, 0:16]), [(PL[1], 0, 1)], [("outb", 0, 16)])
     op("p", mm(T.pb1[:, 0:16], T.yw[0:16, :], T.idh[0:16, 0:16]), [all_("yw"), all_("idh")], [("pb1", 0, 1)])
-    op("v", cp(T.outb[:, 16:32], T.pb1[:, 0:16]), [("pb1", 0, 1)], [("outb", 16, 32)])
+    op("v", cp(T.outp[:], T.pb1[:, 0:16]), [("pb1", 0, 1)], [all_("outp")])
 
-    arrO = send(lambda s: T.outb[:], T.landO[rank], "arrO", "locO", [all_("outb")])
-    dma("y", T.landO[rank], T.outb[:], [all_("outb")], [all_("landO")])
-    dma("y", T.last[:], T.landO[:, rows, 0:16], [all_("landO")], [], [arrO])
-    dma("s", T.peak[:], T.landO[:, rows, 16:32], [all_("landO")], [], [arrO])
+    apart = [p for p in ((0, rank), (rank + 1, 4)) if p[0] < p[1]]
+    for out, buf, land, arr, loc, qs in ((T.last, "outl", "landL", "arrO", "locO", "yy"), (T.peak, "outp", "landP", "arrP", "locP", "sy")):
+        tok = send_all(T[buf][:], T[land][rank], arr, loc, [all_(buf)])
+        dma(qs[0], out[rows, :], T[buf][rows, :], [all_(buf)], [])
+        for q, (r0, r1) in zip(qs, apart):
+            dma(q, out[32 * r0:32 * r1, :], T[land][r0:r1, rows, :], [], [], [tok])
     for sem, val in total.items():
         if known["g"].get(sem, 0) < val:
             g.wait_ge(T.sem[sem], val)

from concourse.bass import DstId, RemoteDMATransfer
from concourse.mybir import AluOpType, ActivationFunctionType

ND = 40
M = 2048
CUTS = (1312, 1312, 1312, 1504)
TURNS = ((0, 0, 6), (2, 6, 12), (2, 6, 12))
HEAD = 320
MASK0 = (0, 6, 12, 16)
LK = (0, 96, 192, 256)
SA = 4
SCRATCH = {
    "srcA": ("dram", [4, 128, 64], "int32"), "srcE": ("dram", [4, 128, 48], "uint16"),
    "landA": ("dram", [4, 128, 64], "int32"), "landE": ("dram", [4, 128, 48], "uint16"),
    "landL": ("dram", [4, 128, 16], "float32"), "landP": ("dram", [4, 128, 16], "float32"),
    "er": ("sbuf", [128, 4, 32], "int32"), "xr": ("sbuf", [128, 16], "int32"), "ed": ("sbuf", [128, 4, 32], "bfloat16"),
    "et": ("sbuf", [128, 4, 32], "bfloat16"), "es": ("sbuf", [128, 4, 16], "bfloat16"), "eu": ("sbuf", [128, 4, 48], "uint16"),
    "xo": ("sbuf", [128, 16], "float32"), "xs": ("sbuf", [128, 16], "float32"),
    "r0": ("sbuf", [128, M], "int32"), "k0": ("sbuf", [128, 512], "float16"),
    "l1r": ("sbuf", [128, 4, 32], "int32"), "l1h": ("sbuf", [128, 4, 64], "float16"), "l1f": ("sbuf", [128, 256], "float16"),
    "t1": ("sbuf", [128, M], "float32"), "t2": ("sbuf", [128, M], "float32"), "tab": ("sbuf", [128, 3 * M], "float32"),
    "ga": ("sbuf", [128, M], "float16"), "gb": ("sbuf", [128, M], "float16"), "gc": ("sbuf", [128, M], "float16"),
    "l1": ("sbuf", [128, 128], "uint16"), "l2": ("sbuf", [128, 128], "uint16"), "l4": ("sbuf", [128, 128], "uint16"), "l8": ("sbuf", [128, 128], "uint16"),
    "ep": ("sbuf", [128, 2, 64], "uint16"), "off": ("sbuf", [128, 2, 64], "float16"), "em": ("sbuf", [128, M], "bfloat16"),
    "ql0": ("sbuf", [128, 16], "uint16"), "ql1": ("sbuf", [128, 16], "uint16"),
    "x0": ("sbuf", [128, 256], "float16"), "x1": ("sbuf", [128, 256], "float16"),
    "z0": ("sbuf", [128, 256], "float16"), "z1": ("sbuf", [128, 256], "float16"),
    "pk": ("sbuf", [128, 256], "float16"), "pk7": ("sbuf", [128, 256], "float16"),
    "yw": ("sbuf", [128, 128], "float16"), "y6": ("sbuf", [128, 128], "float16"),
    "outl": ("sbuf", [128, 16], "float32"), "outp": ("sbuf", [128, 16], "float32"),
    "kq": ("sbuf", [128, 10], "int32"), "kc": ("sbuf", [128, 10], "int32"), "kf": ("sbuf", [128, 10], "float32"), "cf": ("sbuf", [128, 40], "float32"),
    "rm": ("sbuf", [128, 144], "bfloat16"), "r64": ("sbuf", [128, 128], "bfloat16"), "r8": ("sbuf", [128, 16], "bfloat16"),
    "b16": ("sbuf", [128, 16], "float32"), "d64": ("sbuf", [128, 64], "float16"), "idh": ("sbuf", [128, 128], "float16"),
    "mg": ("sbuf", [128, 384], "float16"), "rw": ("sbuf", [128, 576], "float16"), "sw": ("sbuf", [128, 128], "float16"),
    "pm": ("sbuf", [128, 512], "float16"), "seg": ("sbuf", [128, 256], "bfloat16"), "mtab": ("sbuf", [128, 16], "bfloat16"),
}
for _i in range(8):
    SCRATCH["pb%d" % _i] = ("psum", [128, 512], "float32")
SEMAPHORES = ["vv", "ss", "pp", "gq", "arrA", "arrL", "arrE", "arrO", "arrP", "locA", "locL", "locE", "locO", "locP"] + ["d%d" % _i for _i in range(ND)]

ADD, MUL, MAX, MIN = AluOpType.add, AluOpType.mult, AluOpType.max, AluOpType.min
EQ, GE, GT = AluOpType.is_equal, AluOpType.is_ge, AluOpType.is_gt
AND, SHR = AluOpType.bitwise_and, AluOpType.logical_shift_right
AF = ActivationFunctionType


def rank_program(g, core, T, topo):
    rank = T.rank_of(core)
    if rank is None:
        return
    queues = {"v": g.vector, "s": g.scalar, "p": g.tensor, "g": g, "y": g.sync}
    comp = {"v": "vv", "s": "ss", "p": "pp", "g": "gq"}
    total, known, hist, bank, dmas = {}, {q: {} for q in queues}, {}, {}, [0]

    def wait(q, tok):
        sem, val, know = tok
        if known[q].get(sem, 0) < val:
            queues[q].wait_ge(T.sem[sem], val)
            known[q][sem] = val
            for a, b in know.items():
                if known[q].get(a, 0) < b:
                    known[q][a] = b

    def deps(q, reads, writes, is_dma):
        need = []
        for regs, w in ((reads, False), (writes, True)):
            for key, lo, hi in regs:
                if key[:2] == "pb":
                    for oq, tok in bank.get(key, {}).items():
                        if oq != q:
                            need.append(tok)
                    continue
                for l, h, tok, oq, ow in hist.get(key, []):
                    if l < hi and lo < h and (w or ow):
                        same = oq == q and not is_dma
                        if same and w and not ow:
                            continue
                        need.append(tok)
        best = {}
        for tok in need:
            if tok[0] not in best or best[tok[0]][1] < tok[1]:
                best[tok[0]] = tok
        toks = list(best.values())
        for tok in toks:
            if any(o is not tok and o[2].get(tok[0], 0) >= tok[1] for o in toks):
                continue
            wait(q, tok)

    def note(q, tok, reads, writes, is_dma):
        for regs, w in ((reads, False), (writes, True)):
            for key, lo, hi in regs:
                if key[:2] == "pb":
                    bank.setdefault(key, {})[q] = tok
                    continue
                old = hist.setdefault(key, [])
                if w:
                    hist[key] = old = [o for o in old if not (lo <= o[0] and o[1] <= hi)]
                old.append((lo, hi, tok, "dma" if is_dma else q, w))

    def op(q, call, reads, writes, extra=()):
        for tok in extra:
            wait(q, tok)
        deps(q, reads, writes, False)
        sem = comp[q]
        total[sem] = total.get(sem, 0) + 1
        tok = (sem, total[sem], dict(known[q]))
        call(queues[q]).then_inc(T.sem[sem], 1)
        note(q, tok, reads, writes, False)
        return tok

    def dma(q, out, in_, reads, writes, extra=()):
        for tok in extra:
            wait(q, tok)
        deps(q, reads, writes, True)
        sem = "d%d" % dmas[0]
        dmas[0] += 1
        total[sem] = 16
        tok = (sem, 16, dict(known[q]))
        queues[q].dma_start(out, in_).then_inc(T.sem[sem], 16)
        note(q, tok, reads, writes, True)
        return tok

    others = [s for s in range(4) if s != rank]
    far = [s for s in others if topo.die(T.cores[s]) != topo.die(core)]
    SHARE = 4

    def send(src_of, dst, arr, loc, reads, near=1, n=SHARE):
        deps("g", reads, [], True)
        tr = []
        for s in others:
            a = topo.addr(T.cores[s])
            first = 2 * SHARE * far.index(s) if s in far else near
            eng = topo.engines(core, T.cores[s])[first::2][:n]
            tr.append(RemoteDMATransfer(dst_ids=[DstId(rid=a[0], pnc=a[1])], dma_engine_mask=sum(1 << k for k in eng),
                                        remote_sem=T.sem[arr], src=src_of(s), dst=dst))
        g.remote_dma_fused(tr, local_sem=T.sem[loc])
        total[loc] = total[arr] = 3 * n
        return (arr, 3 * n, {})

    def send_all(src, dst, arr, loc, reads):
        deps("g", reads, [], True)
        ads = [topo.addr(T.cores[s]) for s in others]
        n = len(topo.engines(core, T.cores[others[0]]))
        g.remote_dma_fused([RemoteDMATransfer(dst_ids=[DstId(rid=a[0], pnc=a[1]) for a in ads], dma_engine_mask=topo.mask(core, T.cores[others[0]]),
                                              remote_sem=T.sem[arr], srcs=[src], dsts=[dst] * 3)], local_sem=T.sem[loc])
        total[loc], total[arr] = n, 3 * n
        return (arr, 3 * n, {})

    def ts(out, in0, s1, s2, *ops):
        return lambda e: e.tensor_scalar(out, in0, s1, s2, *ops)

    def tt(out, in0, in1, o):
        return lambda e: e.tensor_tensor(out, in0, in1, o)

    def cp(out, in_):
        return lambda e: e.tensor_copy(out, in_)

    def act(out, in_):
        return lambda e: e.activation(out, in_, AF.Copy)

    def move(q, out, in_):
        return act(out, in_) if q == "s" else cp(out, in_)

    def fill(out, c):
        return lambda e: e.memset(out, c)

    def mm(out, lhsT, rhs, start=True, stop=True):
        return lambda e: e.matmul(out, lhsT, rhs, start, stop)

    def iota(out, pattern, base=0, cm=0):
        return lambda e: e.iota(out, pattern, base, cm, allow_small_or_imprecise_dtypes=True)

    def all_(name):
        return (name, 0, 1 << 20)
    W = 128

    A3 = T.srcA
    own = slice(2 * rank, 2 * rank + 2)
    rows = slice(32 * rank, 32 * rank + 32)
    dma("y", A3[:, 0:64, :], T.nx[:], [], [all_("srcAn")])
    dma("s", A3[:, 64:128, :], T.w[:], [], [all_("srcAw")])
    dma("y", T.er[:], T.e[:], [], [all_("er")])
    dma("s", T.xr[:], T.x[:], [], [all_("xr")])
    for s in range(4):
        dma("ys"[s % 2], T.l1r[:, s, :], T.nx[2 * s:2 * s + 2, :], [], [("l1r", s, s + 1)])
    dma("y", T.landA[rank, 0:64, :], T.nx[own, :], [], [all_("landAn")])
    dma("s", T.landA[rank, 64:128, :], T.w[own, :], [], [all_("landAw")])

    op("g", lambda e: e.iota(T.kq[:], [[0, 10]], 0, 1), [], [all_("kq")])
    op("g", iota(T.rm[:], [[1, 144]]), [], [all_("rm")])
    op("g", iota(T.r64[:], [[0, 2], [1, 64]]), [], [all_("r64")])
    op("g", iota(T.r8[:], [[0, 2], [1, 8]]), [], [all_("r8")])
    arrA = send(lambda s: A3[s], T.landA[rank], "arrA", "locA", [all_("srcAn"), all_("srcAw")], 1, SA)

    kf, cf = T.kf, T.cf
    op("v", fill(T.seg[:], 1.0), [], [all_("seg")])
    op("v", fill(T.eu[:], 0), [], [all_("eu")])
    op("v", fill(T.seg[:, 0:256:16], 0.0), [], [all_("seg")])
    PF = [(AND, 127), (AND, 15), (AND, 112), (SHR, 4, AND, 1), (SHR, 4), (AND, 7), (SHR, 3, AND, 1), (AND, 63), (SHR, 6)]
    for i, f in enumerate(PF):
        kc, kq = T.kc[:, i:i + 1], T.kq[:, i:i + 1]
        op("v", ts(kc, kq, f[1], None, f[0]) if len(f) == 2 else ts(kc, kq, f[1], f[3], f[0], f[2]), [all_("kq")], [("kc", i, i + 1)])
    op("v", cp(kf[:, 0:9], T.kc[:, 0:9]), [all_("kc")], [all_("kf")])
    KF, RM = all_("kf"), all_("rm")
    names = {}

    def col(n):
        return kf[:, n:n + 1] if n in range(10) else cf[:, names[n]:names[n] + 1]

    def ck(*ns):
        return [KF] + [("cf", names[n], names[n] + 1) for n in ns if n in names]

    def cts(n, in0, s1, s2, *ops):
        args = [a if a is None or isinstance(a, float) else col(a) for a in (in0, s1, s2)]
        rd = ck(in0, s1, s2)
        names[n] = len(names)
        op("v", ts(col(n), args[0], args[1], args[2], *ops), rd, ck(n)[1:])

    def match(out, okey, row, rkey, at, on=None):
        if on is None:
            op("v", ts(out, row, col(at), None, EQ), [rkey] + ck(at), [okey])
        else:
            op("v", ts(out, row, col(at), col(on), EQ, MUL), [rkey] + ck(at, on), [okey])

    STEP = ((1, 1.0), (2, 2.0), (4, 3.5))
    cts("row0", 1, 0.0, None, EQ)
    cts("ja", 6, -7.5, 1, MUL, ADD)
    cts("c15", 2, 15.0, None, ADD)
    cts("lo8", 6, -1.0, 1.0, MUL, ADD)
    op("v", ts(T.b16[:], T.rm[:, 0:16], 128.0, col("row0"), MUL, MUL), [RM] + ck("row0"), [all_("b16")])
    for j in range(16):
        op("s", lambda e, j=j: e.activation(T.r0[:, W * j:W * j + W], T.rm[:, 0:W], AF.Identity, bias=T.b16[:, j:j + 1], scale=col("row0")),
           [RM, all_("b16")] + ck("row0"), [("r0n", j, j + 1), ("r0w", j, j + 1)])
    cts("jc", "row0", 100.0, "ja", MUL, ADD)
    cts("na", 2, 96.0, -128.0, GE, MUL)
    cts("sa", 4, 8.0, 5, MUL, ADD)
    cts("pa", 5, 16.0, 4, MUL, ADD)
    cts("ta", 5, 6, None, ADD)
    cts("y0", 3, -1.0, 1.0, MUL, ADD)
    cts("h0", 8, -1.0, 1.0, MUL, ADD)
    match(T.d64[:], all_("d64"), T.r64[:, 0:64], all_("r64"), 7)
    for i, (s, thr) in enumerate(STEP):
        cts("ra%d" % i, 1, float(s), None, EQ)
        cts("ma%d" % i, "jc", thr, -1000.0, GT, MUL)
    match(T.idh[:], all_("idh"), T.rm[:, 0:W], RM, 0)

    op("v", ts(T.ed[:, :, 0:16], T.er[:, :, 16:32], col("y0"), None, MUL), [all_("er")] + ck("y0"), [("ed", 0, 1)])
    op("v", ts(T.ed[:, :, 16:32], T.er[:, :, 16:32], col(3), None, MUL), [all_("er"), KF], [("ed", 1, 2)])
    op("v", ts(T.xo[:], T.er[:, 0, 0:16], 8, M, GE, MUL), [all_("er")], [all_("xo")])
    op("v", cp(T.eu[:, :, 0:16], T.er[:, :, 0:16]), [all_("er")], [("eu", 0, 1)])
    op("v", lambda e: e.transpose(T.et[:], T.ed[:]), [all_("ed")], [all_("et")])
    op("v", tt(T.xs[:], T.xo[:], T.xr[:], ADD), [all_("xo"), all_("xr")], [all_("xs")])
    op("v", tt(T.es[:], T.et[:, :, 0:16], T.et[:, :, 16:32], ADD), [all_("et")], [all_("es")])
    op("v", cp(T.eu[:, 0, 32:48], T.xs[:]), [all_("xs")], [("eu", 1, 2)])
    op("v", cp(T.eu[:, :, 16:32], T.es[:]), [all_("es")], [("eu", 2, 3)])
    dma("y", T.srcE[:], T.eu[:], [all_("eu")], [all_("srcE")])
    dma("y", T.landE[rank], T.eu[rows, :, :], [all_("eu")], [all_("landE")])

    for c in range(2):
        for y in range(2):
            o = 32 * y + c
            op("v", ts(T.l1h[:, :, o:32 * y + 32:2], T.l1r[:, :, 16 * c:16 * c + 16], col(("h0", 8)[y]), None, MUL), [all_("l1r")] + ck("h0"), [("l1h", o, o + 1)])
    mine = T.l1f[:, 64 * rank:64 * rank + 64]
    arrL = send(lambda s: T.l1h[:, s, :], mine, "arrL", "locL", [all_("l1h")])
    arrE = send(lambda s: T.srcE[s], T.landE[rank], "arrE", "locE", [all_("srcE")], 2 * SHARE + 1)

    cts("nb", "na", 2, 47.0, ADD, ADD)
    cts("pb", "pa", 8.0, None, ADD)
    cts("tb", "lo8", 100.0, "ta", MUL, ADD)
    op("v", cp(mine, T.l1h[:, rank, :]), [all_("l1h")], [all_("l1f")])
    for i, (s, thr) in enumerate(STEP):
        cts("mb%d" % i, "ma%d" % i, 0, float(s), ADD, ADD)
        match(T.rw[:, 144 * i:144 * i + 144], ("rw", i, i + 1), T.rm[:], RM, "c15", "ra%d" % i)
    match(T.sw[:], all_("sw"), T.r64[:], all_("r64"), "sa", 6)
    match(T.rw[:, 432:576], ("rw", 3, 4), T.rm[:], RM, "nb", "lo8")
    for i in range(3):
        match(T.mg[:, W * i:W * i + W], ("mg", i, i + 1), T.rm[:, 0:W], RM, "mb%d" % i)
    for h in range(2):
        for h2 in range(2):
            i = 2 * h + h2
            match(T.pm[:, W * i:W * i + W], ("pm", i, i + 1), T.rm[:, 0:W], RM, ("pa", "pb")[h], ("lo8", 6)[h2])
    op("v", ts(T.mtab[:], T.r8[:], col("tb"), col("ta"), MIN, EQ), [all_("r8")] + ck("ta", "tb"), [all_("mtab")])

    R0K = [all_("r0n"), all_("r0w")]
    dma("y", T.r0[1:128:16, :], T.landA[:, 0:64, :], [all_("landAn")], R0K[:1], [arrA])
    dma("s", T.r0[8:128:16, :], T.landA[:, 64:128, :], [all_("landAw")], R0K[1:], [arrA])
    op("g", lambda e: e.affine_select(T.k0[:], T.r0[:, 512:1024], [[0, 512]], GE, 0.0, 0, 0), R0K, [all_("k0")])
    op("g", iota(T.tab[:, 0:M], [[0, M]]), [], [("tab", 0, M)])
    for t in range(4):
        for r0, r1, sh in ((0, 4 - t, t), (4 - t, 4, t - 4)):
            if r0 < r1:
                dma("y", T.ep[32 * (r0 + sh):32 * (r1 + sh), :, 16 * t:16 * t + 16],
                    T.landE[r0:r1, t // 2::2, 16 * (t % 2):16 * (t % 2) + 16], [all_("landE")], [("ep", 2 * t + (r0 > 0), 2 * t + (r0 > 0) + 1)], [arrE])
    dma("y", T.ql0[:], T.landE[:, 0::4, 32:48], [all_("landE")], [all_("ql0")], [arrE])

    for c in range(2):
        op("p", mm(T.pb6[:, c:W:2], T.l1f[:, c:256:2], T.d64[:]), [all_("l1f"), all_("d64")], [("pb6", 0, 1)], [arrL])
    op("v", cp(T.l1[:], T.pb6[:, 0:W]), [("pb6", 0, 1)], [all_("l1")])

    TB, GK = ["pb0", "pb1", "pb2", "pb3"], ["ga", "gb", "gc"]

    def gather(q, out, okey, o0, lo, hi, win, wkeys, lst):
        op(q, move(q, out[:, o0 + lo:o0 + hi], win.indirect(T[lst][:, lo // 16:hi // 16])),
           wkeys + [(lst, lo // 16, hi // 16)], [(okey, o0 + lo, o0 + hi)])

    def relist(h, lst, q="v"):
        b = "pb%d" % (4 + h)
        op(q, move(q, T[lst][:, 64 * h:64 * h + 64], T[b][:, 0:64]), [(b, 0, 1)], [(lst, 64 * h, 64 * h + 64)])

    def mask(t, lo=0, hi=16):
        c, o = t % 4, 256 * t
        op("s", act(T.em[:, o + 16 * lo:o + 16 * hi], T.mtab[:].indirect(T.ep[:, t // 4, 16 * c + lo:16 * c + hi])),
           [all_("mtab"), ("ep", 2 * c, 2 * c + 2)], [("em", o + 16 * lo, o + 16 * hi)])

    def level(i, win, wkeys, lst, dst, d0, nxt):
        gk, CUT, (R0, R1, R2) = GK[i], CUTS[i], TURNS[i]

        def piece(q, lo, hi):
            gather(q, T[gk], gk, 0, lo, hi, T[win][:], wkeys, lst)

        def merge(lo, hi, start=True, stop=True, j=i):
            c = lo // 512
            op("p", mm(T[TB[c]][:, lo - 512 * c:hi - 512 * c], T.mg[:, W * j:W * j + W], T[GK[j]][:, lo:hi], start, stop),
               [("mg", j, j + 1), (GK[j], lo, hi)], [(TB[c], 0, 1)])

        def relay(h, r0=0, r1=16):
            b = "pb%d" % (4 + h)
            for r in range(r0, r1):
                op("p", mm(T[b][:, 0:64], T.rw[:, 144 * i + 15 - r:144 * i + 143 - r], T[gk][:, 1024 * h + r:1024 * h + 1024:16], r == 0, r == 15),
                   [("rw", i, i + 1), (gk, 1024 * h, 1024 * h + 1024)], [(b, 0, 1)])

        def out(lo, hi):
            c = lo // 512
            op("v", tt(T[dst][:, d0 + lo:d0 + hi], T[win][:, lo:hi], T[TB[c]][:, lo - 512 * c:hi - 512 * c], ADD),
               [(TB[c], 0, 1)] + wkeys, [(dst, d0 + lo, d0 + hi)])

        def old():
            op("p", mm(T.pb1[:], T.idh[:], T.k0[:], i > 0, i == 0), [all_("idh"), all_("k0")], [("pb1", 0, 1)])
            for j in range(i):
                merge(512, 1024, False, False, j)
        head = HEAD if i else 512
        piece("v", 0, head)
        piece("s", 512, 1024)
        if i:
            relist(1, lst)
            piece("v", head, 512)
        piece("v", 1024, CUT)
        piece("s", 1536, M)
        piece("s", CUT, 1536)
        if i:
            old()
        merge(0, head)
        if i:
            merge(head, 512)
        merge(512, 1024, i == 0, i > 0)
        relay(0, 0, R0)
        merge(1024, CUT)
        if not i:
            old()
        out(0, 512)
        out(1024, CUT)
        if i == 2:
            op("v", ts(T.off[:], T.ep[:], 8, M, GE, MUL), [all_("ep")], [all_("off")])
        relay(0, R0, R1)
        merge(1536, M)
        relay(0, R1, R2)
        merge(CUT, 1536)
        relay(0, R2, 16)
        op("s", act(T[dst][:, d0 + 512:d0 + 1024], T.pb1[:]), [("pb1", 0, 1)], [(dst, d0 + 512, d0 + 1024)])
        out(1536, M)
        if not i:
            mask(0, MASK0[i], MASK0[i + 1])
        relist(0, nxt, "s")
        if i:
            mask(0, MASK0[i], MASK0[i + 1])
        out(CUT, 1536)
        relay(1)

    level(0, "r0", R0K, "l1", "t1", 0, "l2")
    level(1, "t1", [all_("t1")], "l2", "t2", 0, "l4")
    level(2, "t2", [all_("t2")], "l4", "tab", M, "l8")
    A, AK = T.tab[:, M:2 * M], [("tab", M, 2 * M)]
    gather("v", T.tab, "tab", 2 * M, 0, HEAD, A, AK, "l8")
    gather("s", T.tab, "tab", 2 * M, 512, 1024, A, AK, "l8")
    relist(1, "l8")
    gather("v", T.tab, "tab", 2 * M, HEAD, 512, A, AK, "l8")
    gather("v", T.tab, "tab", 2 * M, 1024, CUTS[3], A, AK, "l8")
    gather("s", T.tab, "tab", 2 * M, CUTS[3], M, A, AK, "l8")

    PL, PW = ["pb4", "pb5"], ["pb6", "pb7"]

    def look(t, h):
        q, x, lo, hi = "ql%d" % (t % 2), "x%d" % (t % 2), LK[h], LK[h + 1]
        op("v", tt(T[x][:, lo:hi], T.tab[:, M:3 * M].indirect(T[q][:, lo // 16:hi // 16]), T.em[:, 256 * t + lo:256 * t + hi], MUL),
           [("tab", M, 3 * M), all_(q), ("em", 256 * t + lo, 256 * t + hi)], [(x, lo, hi)])

    def early(t):
        q, z = "ql%d" % (t % 2), "z%d" % (t % 2)
        op("s", act(T[z][:], T.tab[:, 0:2 * M].indirect(T[q][:])), [("tab", 0, 2 * M), all_(q)], [all_(z)])

    def places(t, h):
        x, b = "x%d" % (t % 2), PL[t % 2]
        if h == 0 and t < 7:
            n = t + 1
            op("p", mm(T[b][:, 0:16], T.idh[:], T.off[:, n // 4, 16 * (n % 4):16 * (n % 4) + 16], True, False), [all_("idh"), all_("off")], [(b, 0, 1)])
        for a in range(LK[h] // 16, LK[h + 1] // 16):
            op("p", mm(T[b][:, 0:16], T.rw[:, 447 - a:575 - a], T[x][:, 16 * a:16 * a + 16], t == 7 and a == 0, a == 15),
               [("rw", 3, 4), (x, LK[h], LK[h + 1])], [(b, 0, 1)])

    def wz(t, h):
        z, b, c, o = "z%d" % (t % 2), PW[t % 2], 16 * (t % 4), W * h
        op("p", mm(T[b][:, o + 1:o + W:2], T[z][:, o:o + W], T.sw[:, c:c + 64]), [all_(z), all_("sw")], [(b, 0, 1)])

    def wx(t, h):
        x, b, c, o = "x%d" % (t % 2), PW[t % 2], 16 * (t % 4), W * h
        carry = 0 < t < 7
        op("p", mm(T[b][:, o:o + W:2], T[x][:, o:o + W], T.sw[:, c:c + 64], True, not carry), [(x, o, o + W), all_("sw")], [(b, 0, 1)])
        if carry:
            for h0 in range(2):
                i = 2 * h0 + h
                op("p", mm(T[b][:, o + 14:o + W:16], T.pm[:, W * i:W * i + W], T.pk[:, W * h0 + 15:W * h0 + W:16], False, h0 == 1),
                   [("pm", i, i + 1), all_("pk")], [(b, 0, 1)])

    def scan(t):
        b, pk = PW[t % 2], "pk7" if t == 7 else "pk"
        op("v", lambda e: e.tensor_tensor_scan(T[pk][:], T.seg[:], T[b][:, 0:256], 0.0, MUL, MAX), [all_("seg"), (b, 0, 1)], [all_(pk)])

    for t in range(7):
        early(t)
        for h in range(3):
            look(t, h)
            places(t, h)
        mask(t + 1)
        if t > 0:
            scan(t - 1)
        wz(t, 0)
        wz(t, 1)
        wx(t, 0)
        wx(t, 1)
        b, q = PL[t % 2], "ql%d" % ((t + 1) % 2)
        op("v", cp(T[q][:], T[b][:, 0:16]), [(b, 0, 1)], [all_(q)])
    early(7)
    for h in range(3):
        look(7, h)
    places(7, 0)
    places(7, 1)
    wz(7, 0)
    wz(7, 1)
    wx(7, 0)
    wx(7, 1)
    places(7, 2)
    scan(6)
    scan(7)
    op("s", act(T.outl[:], T[PL[1]][:, 0:16]), [(PL[1], 0, 1)], [all_("outl")])
    for r in range(16):
        for h in range(2):
            o = W * (2 * h + r // 8) + 16 * (r % 8)
            op("p", mm(T.pb2[0:16, r:W:16], T.pm[:, o:o + 16], T.pk[:, W * h + 15:W * h + W:16], h == 0, h == 1), [all_("pm"), all_("pk")], [("pb2", 0, 1)])
    op("s", act(T.y6[0:16, :], T.pb2[0:16, 0:W]), [("pb2", 0, 1)], [all_("y6")])
    for h in range(2):
        for r in range(8):
            op("p", mm(T.pb0[0:16, 8 * h + r:W:16], T.idh[:, 16 * r:16 * r + 16], T.pk7[:, W * h + 15:W * h + W:16]), [all_("idh"), all_("pk7")], [("pb0", 0, 1)])
    op("v", tt(T.yw[0:16, :], T.y6[0:16, :], T.pb0[0:16, 0:W], MAX), [("pb0", 0, 1), all_("y6")], [all_("yw")])
    op("p", mm(T.pb1[:, 0:16], T.yw[0:16, :], T.idh[0:16, 0:16]), [all_("yw"), all_("idh")], [("pb1", 0, 1)])
    op("v", cp(T.outp[:], T.pb1[:, 0:16]), [("pb1", 0, 1)], [all_("outp")])

    apart = [p for p in ((0, rank), (rank + 1, 4)) if p[0] < p[1]]
    for out, buf, land, arr, loc, qs in ((T.last, "outl", "landL", "arrO", "locO", "yy"), (T.peak, "outp", "landP", "arrP", "locP", "sy")):
        tok = send_all(T[buf][:], T[land][rank], arr, loc, [all_(buf)])
        dma(qs[0], out[rows, :], T[buf][rows, :], [all_(buf)], [])
        for q, (r0, r1) in zip(qs, apart):
            dma(q, out[32 * r0:32 * r1, :], T[land][r0:r1, rows, :], [], [], [tok])
    for sem, val in total.items():
        if known["g"].get(sem, 0) < val:
            g.wait_ge(T.sem[sem], val)
